import numpy as np, ml_dtypes
CORES = [1,5,17,21,33,37,49,53]
N = 8
import mx_ref
BF = ml_dtypes.bfloat16
def entries(a):
    return np.ascontiguousarray(a.T).reshape(-1)
def table(e):
    return np.ascontiguousarray(np.reshape(e, (-1, 16)).T).astype(np.int32)
def cols(t, e):
    v = np.concatenate([t.reshape(128, -1, 4), np.zeros((128, 1, 4), BF)], axis=1)
    return np.ascontiguousarray(v[:, e]).reshape(128, -1)
def cut(t, i, w=512):
    return t[:, w * i:w * i + w]
def f(rng, *shape):
    return mx_ref.flush((rng.standard_normal(shape, dtype=np.float32) * np.exp2(rng.integers(-2, 3, shape[:-1] + (1,)))).astype(BF))
def wide(rng, *shape, cols=0):
    v = rng.standard_normal(shape, dtype=np.float32) * np.exp2(rng.integers(-12, 13, shape)).astype(np.float32)
    if cols: v *= np.repeat(np.exp2(rng.integers(-cols, cols + 1, shape[:-2] + (1, shape[-1] // 4))) * (rng.random(shape[:-2] + (1, shape[-1] // 4)) > 0.0625), 4, axis=-1).astype(np.float32)
    return mx_ref.flush(v.astype(BF))
C, P, B, O, DN, DS = 192, 384, 3, 2, 224, 112
def lists(rng, S, straddle=0.5, fill="any", flip=None):
    o = np.array([[max(0, min(S[r + 1], P * q + P) - max(S[r], P * q)) for q in range(N)] for r in range(N)])
    ends, both = np.zeros((N, N), int), {}
    for r in range(N):
        for q in range(N - 1):
            if o[r, q] > 0 and o[r, q + 1] > 0 and rng.random() < straddle:
                a = int(rng.integers(1, min(5, o[r, q]) + 1))
                b = int(rng.integers(1, min(6 - a, o[r, q + 1]) + 1))
                if fill == "few":
                    a = int(o[r, q] % 6); b = 6 - a
                    if a == 0: continue
                o[r, q] -= a; o[r, q + 1] -= b
                ends[r, q] += 1; ends[r, q + 1] += 1; both[r, q] = a + b
    K = np.floor_divide(o + 5, 6)
    segs = [(r, q) for r in range(N) for q in range(N) if o[r, q] > 0]
    segs = [segs[i] for i in rng.permutation(len(segs))]
    if fill == "full": segs = [s for s in segs if s[1] % 2 == 1] + [s for s in segs if s[1] % 2 == 0]
    if fill == "few": segs = []
    for r, q in segs:
        room = int(min(DS - ends[r, q] - K[r, q], o[r, q] - K[r, q], C - (ends[r].sum() >> 1) - K[r].sum(), DN - ends[:, q].sum() - K[:, q].sum()))
        K[r, q] += room if fill == "full" else rng.integers(0, room + 1)
    m = np.zeros((N, C), int)
    for r in range(N):
        e = []
        for q in range(N):
            k = int(K[r, q])
            e += (1 + np.bincount(rng.permutation(np.repeat(np.arange(k), 5))[:o[r, q] - k], minlength=k)).tolist()
            if (r, q) in both: e.append(both[r, q])
        m[r, np.sort(rng.permutation(C)[:len(e)])] = np.array(e, int)
    if flip is None: flip = rng.random() < 0.5
    if flip: m = m[::-1, ::-1]
    return {"cnt": np.stack([table(e) for e in m])}
def begins(rng):
    for k in range(50):
        S, e = [0], 1 - 2 * int(rng.integers(2))
        turn = N if rng.random() < 0.5 else int(rng.integers(2, N))
        for r in range(1, N):
            if r == turn: e = -e
            s = S[-1] - P * (r - 1)
            lo = max(s - P, -2 * P, -((3 * P * (N - r)) >> 1))
            hi = min(s + ((3 * P) >> 1), 2 * P, P * (N - r))
            a, b = (max(lo, (3 * P) >> 2), hi) if e > 0 else (lo, min(hi, -((3 * P) >> 2)))
            if a > b: a = b = hi if e > 0 else lo
            S.append(P * r + int(rng.integers(a, b + 1)))
        S.append(N * P)
        own = sum(max(0, min(S[r + 1], P * r + P) - max(S[r], P * r)) for r in range(N))
        if 2 * own <= N * P: return S
    raise RuntimeError("begins")
def floats(rng):
    return {"x": f(rng, N, 128, 4 * C), "w": f(rng, N, 128, 512 * B * O)}
def setup_inputs(rng):
    return {**floats(rng), **lists(rng, begins(rng))}
def setup_inputs_full(rng):
    S = [0] + [P * r + (P >> 1) + int(rng.integers(-(P >> 4), (P >> 4) + 1)) for r in range(1, N)] + [N * P]
    return {**floats(rng), **lists(rng, S, straddle=2.0, fill="full")}
def setup_inputs_furthest(rng):
    S = [0] + [min(P * (r + 2), N * P) for r in range(1, N + 1)]
    return {**floats(rng), **lists(rng, S, straddle=2.0, fill="few")}
def setup_inputs_dense(rng):
    def some(k, n):
        return (1 + np.bincount(rng.permutation(np.repeat(np.arange(k), 5))[:n - k], minlength=k)).tolist()
    H = min(P // 256 * 128 + 64, P - DS) if N > 4 else (P - 1) // 256 * 128 + 64
    X = (7 * DS - P) // 5
    flip = bool(rng.random() < 0.5)
    front = 3 + 2 * int(rng.integers((N - 2) // 2))
    e = [[] for r in range(N)]
    for q in range(2, N):
        h, i, j = P // 2, 0, 0
        if q == front: h, i, j = (P - DS, X, DS) if flip else (DS, DS, X)
        elif q % 2 == 1 or N == 4: h, i, j = H, H % 128, 128 - H % 128
        a, b = h - i, P - h - j
        if q == 2: a += 2 * P
        if q % 2 == 1: ka, kb = DS - i, DS - j
        else:
            ka = int(rng.integers(-(-a // 6), (C if q == 2 else C - DS) - i + 1))
            kb = int(rng.integers(-(-b // 6), C - DS - j + 1))
        e[q - 2] += some(ka, a) + [1] * i
        e[q - 1] += [1] * j + some(kb, b)
    m = np.zeros((N, C), int)
    for r in range(N):
        m[r, np.sort(rng.permutation(C)[:len(e[r])])] = np.array(e[r], int)
    if flip: m = m[::-1, ::-1]
    return {**floats(rng), "cnt": np.stack([table(v) for v in m])}
def setup_inputs_many(rng):
    def some(k, n):
        return (1 + np.bincount(rng.permutation(np.repeat(np.arange(k), 5))[:n - k], minlength=k)).tolist()
    src = [[0], [0, 1, 2, 3], [3], [3]] if N == 4 else [[0], [0], [0, 1, 2, 3, 4], [4], [4], [4, 5, 6, 7], [7], [7]]
    flip = bool(rng.random() < 0.5)
    lo = -(-P // 6)
    alone = [src.count([r]) for r in range(N)]
    among = [sum(len(s) > 1 and r in s for s in src) for r in range(N)]
    least = [alone[r] * lo + (1 - among[r] - alone[r] * lo) % N for r in range(N)]
    k = np.zeros((N, N), int)
    for q, s in enumerate(src):
        if len(s) == 1: continue
        c = np.ones(len(s), int)
        c[int(rng.integers(1, len(s) - 1))] = N - len(s) + 1
        top = np.array([(min(DS, (C - least[r]) // among[r]) - int(c[i])) // N for i, r in enumerate(s)])
        j = np.ones(len(s), int)
        while j.sum() < DN // N - 1: j[int(rng.choice(np.flatnonzero(j < top)))] += 1
        k[s, q] = N * j + c
    for r in range(N):
        n = alone[r]
        if n == 0: continue
        z = min(C - int(k[r].sum()), n * DS)
        w = least[r] + N * int(rng.integers(0, (z - least[r]) // N + 1))
        for q in range(N):
            if src[q] == [r]:
                n -= 1
                u = int(rng.integers(max(lo, w - DS * n), min(DS, w - lo * n) + 1))
                k[r, q] = u; w -= u
    e = [[] for r in range(N)]
    for q, s in enumerate(src):
        v = some(int(k[:, q].sum()), P)
        for r in s:
            i = int(k[r, q])
            e[r] += v[:i]; v = v[i:]
    m = np.zeros((N, C), int)
    for r in range(N):
        m[r, np.sort(rng.permutation(C)[:len(e[r])])] = np.array(e[r], int)
    if flip: m = m[::-1, ::-1]
    return {**floats(rng), "cnt": np.stack([table(v) for v in m])}
def setup_inputs_spread(rng):
    d = setup_inputs(rng); v = np.array(wide(rng, N, 128, 4 * C, cols=6))
    v[np.abs(v.astype(np.float32)) < 2.0 ** -30] = 0
    d["x"] = v; return d
def check_inputs(d):
    b = []
    for k in ("x", "w"):
        v = np.abs(d[k].astype(np.float32))
        if not ((v == 0) | ((v >= 2.0 ** -30) & (v <= 2.0 ** 30))).all(): b.append("the range of " + k)
    m = np.stack([entries(a) for a in d["cnt"]])
    if m.min() < 0 or m.max() > 6: return b + ["cnt"]
    if m.sum() != N * P: return b + ["the sum of all counts"]
    runs = np.repeat(np.arange(N * C), m.reshape(-1)).reshape(N, P)
    for q in range(N):
        u = np.unique(runs[q])
        k = np.bincount(np.floor_divide(u, C), minlength=N)
        if len(u) > DN: b.append("different columns in a run")
        if k.max() > DS: b.append("different columns of one rank in a run")
        if (np.abs(np.flatnonzero(k) - q) > 2).any(): b.append("a column of a rank more than two away")
    return b
def reference(x, w, cnt):
    m = np.stack([entries(a) for a in cnt])
    runs = np.repeat(np.arange(N * C), m.reshape(-1)).reshape(N, P)
    t = np.concatenate([x[r] for r in range(N)], axis=1)
    y = np.zeros((N, 128, O * P), np.float32)
    for q in range(N):
        for b in range(B):
            c = mx_ref.quantize(cols(t, runs[q, 128 * b:128 * b + 128]))
            for o in range(O):
                i = P * o + 128 * b
                y[q][:, i:i + 128] = mx_ref.matmul(mx_ref.quantize(cut(w[q], O * b + o)), c)
    return {"y": y}

@@ -1,0 +1,344 @@
+from concourse.bass import DstId, RemoteDMATransfer
+from concourse.mybir import dt, AluOpType as Op, AxisListType, ActivationFunctionType as Act
+
+C, P, NB, NO, H = 192, 384, 3, 2, 112
+W0 = 1536
+TR = 2048
+BIG = 1.0e6
+WIN = 3 * H + 2 * C
+F32, I32, U16, U8, F8, BF = "float32", "int32", "uint16", "uint8", "float8_e4m3fn_x4", "bfloat16"
+
+
+def sb(n, t):
+    return ("sbuf", [128, n], t)
+
+
+SCRATCH = {
+    "xt": sb(4 * C, BF), "wt": sb(512 * 6, BF), "wq": sb(768, F8), "ws": sb(768, U8),
+    "raw": sb(C, F8), "raws": sb(C, U8), "comp": sb(C, F8), "comps": sb(C, U8),
+    "sel2": sb(H, F8), "sel2s": sb(H, U8), "selz": sb(H, F8), "selzs": sb(H, U8),
+    "win": sb(WIN, F8), "wins": sb(WIN, U8), "fin": sb(P, F8), "fins": sb(P, U8),
+    "pi": sb(1, I32), "pa": sb(1, I32), "pf": sb(1, F32), "p12": sb(1, F32), "c16": sb(16, F32), "c1": sb(16, F32),
+    "tj": sb(16, F32), "tj192": sb(16, F32), "tjtr": sb(16, F32), "m2": sb(16, F32), "ord": sb(12, U16),
+    "ir": sb(WIN, F32), "mi": sb(P, I32), "mj": sb(P, I32), "mask": sb(P, F32), "rm": sb(128, F32), "cb": sb(8, F32),
+    "tb": sb(12, I32), "row1": sb(C, I32), "rowi": sb(C, I32), "T1": sb(128, F32), "A1": sb(128, F32), "B1": sb(128, F32),
+    "Z1": sb(128, F32), "cc": sb(16, F32), "cn": sb(16, F32), "z0": sb(12, F32), "z1": sb(12, F32), "z2": sb(12, F32),
+    "o1": sb(12, F32), "o2": sb(12, F32), "ok": sb(12, U16), "kr": sb(2 * C, F32), "kd": sb(C, F32),
+    "kl": sb(12, U16), "ke": sb(12, U16), "cr": sb(C, F32), "er": sb(2 * C, F32), "sc": sb(C, F32),
+    "s1": sb(12, F32), "s2": sb(12, F32), "sx": sb(12, F32), "sxu": sb(12, U16),
+    "f2": sb(1, F32), "l2": sb(8, U16), "r2": sb(H, F32), "d0": sb(H, F32), "d2": sb(H, F32), "dz": sb(H, F32),
+    "t0": sb(8, U16), "t2": sb(8, U16), "tz": sb(8, U16), "rz": sb(H, F32),
+    "tl": sb(8, F32), "S": sb(1, F32), "bc": sb(8, F32), "pc": sb(1, F32), "jk": sb(C, F32), "acc": sb(1, F32), "fz": sb(1, F32),
+    "lz": sb(8, U16), "pt": sb(12, U16), "po": sb(12, U16), "oo": sb(12, U16), "ct": sb(24, U16),
+    "pw": sb(6144, F32), "pm": sb(P + 16, F32), "pd": sb(P, F32), "il": sb(24, U16),
+    "ysb": sb(NO * P, F32), "ps": ("psum", [128, 512 * 6], F32),
+}
+SEMAPHORES = ["sv", "sa", "sg", "st", "dtab", "drow", "dx", "dw0", "dw1", "down", "dy", "sent",
+              "atot", "apt", "apc", "act", "acd"]
+
+
+def common(topo, src, dsts):
+    e = topo.engines(src, dsts[0])
+    for d in dsts[1:]:
+        e = [k for k in e if k in topo.engines(src, d)]
+    return e
+
+
+def groups(e, k):
+    n = len(e)
+    if k == 1:
+        return [e]
+    if k == 2:
+        return [e[:n // 2], e[n // 2:]]
+    return [e[:n // 4], e[n // 4:n // 2], e[n // 2:]]
+
+
+def bits(e):
+    m = 0
+    for k in e:
+        m |= 1 << k
+    return m
+
+
+def rank_program(g, core, T, topo):
+    r = T.rank_of(core)
+    if r is None:
+        return
+    cores = T.cores
+    N = len(cores)
+
+    def partner(q):
+        return [d for d in (q - 1, q + 1) if 0 <= d < N and topo.chip(cores[d]) == topo.chip(cores[q])][0]
+
+    def off(q):
+        v = [("m2", q - 2), ("p2", q + 2)] + [("z", d) for d in (q - 1, q + 1) if d != partner(q)]
+        return [(k, d) for k, d in v if 0 <= d < N]
+
+    def seg(d):
+        a, o = {}, 0
+        for s in range(d - 2, d + 3):
+            if 0 <= s < N:
+                n = C if s in (d, partner(d)) else H
+                a[s] = (o, n)
+                o += n
+        return a
+
+    def masks(q, kinds):
+        ks = [(k, d) for k, d in off(q) if k in kinds]
+        if not ks:
+            return {}
+        return dict(zip([k for k, d in ks], groups(common(topo, cores[q], [cores[d] for k, d in ks]), len(ks))))
+
+    pt = partner(r)
+    me = seg(r)
+    dest = dict(off(r))
+    qs = {"v": g.vector, "a": g.scalar, "s": g.sync, "t": g.tensor, "g": g}
+    home = {"v": "sv", "a": "sa", "t": "st", "g": "sg"}
+    seen, total = {}, {}
+
+    def need(q, toks):
+        for sem, val in toks:
+            if seen.get((q, sem), 0) < val:
+                qs[q].wait_ge(T.sem[sem], val)
+                seen[(q, sem)] = val
+
+    def do(q, deps, fn, sem=None, n=1):
+        need(q, deps)
+        s = sem or home[q]
+        fn().then_inc(T.sem[s], n)
+        total[s] = total.get(s, 0) + n
+        return (s, total[s])
+
+    V, A = g.vector, g.scalar
+
+    def dma(q, sem, out, in_, deps=()):
+        return do(q, deps, lambda: qs[q].dma_start(out, in_), sem, 16)
+
+    def dst(c):
+        rid, pid, _ = topo.addr(c)
+        return DstId(rid=rid, pnc=pid)
+
+    sent = [0]
+
+    def fused(deps, trs):
+        need("g", deps)
+        g.remote_dma_fused([RemoteDMATransfer(dst_ids=[dst(cores[d]) for d in ds], dma_engine_mask=bits(e), remote_sem=T.sem[sem],
+                                              srcs=[a], dsts=[b] * len(ds)) for ds, e, sem, a, b in trs], local_sem=T.sem.sent)
+        sent[0] += sum(len(e) for ds, e, sem, a, b in trs)
+
+    def tc(deps, out, in_):
+        return do("v", deps, lambda: V.tensor_copy(out, in_))
+
+    def tt(deps, out, a, b, op):
+        return do("v", deps, lambda: V.tensor_tensor(out, a, b, op))
+
+    def ts(deps, out, a, s1, op0, s2=None, op1=None):
+        if op1 is None:
+            return do("v", deps, lambda: V.tensor_scalar(out, a, s1, None, op0))
+        return do("v", deps, lambda: V.tensor_scalar(out, a, s1, s2, op0, op1))
+
+    def scan(deps, out, a, b, init, op0, op1):
+        return do("v", deps, lambda: V.tensor_tensor_scan(out, a, b, init, op0, op1))
+
+    def fill(ap, c):
+        return do("v", (), lambda: V.memset(ap, c))
+
+    def act(deps, out, in_, func=Act.Copy, **kw):
+        return do("a", deps, lambda: A.activation(out, in_, func, **kw))
+
+    def pick(deps, out, in_, o):
+        return tc(deps, out.bitcast(dt.uint32), in_.bitcast(dt.uint32).indirect(o))
+
+    drow = dma("s", "drow", T.row1[0:1, :], T.cnt[:])
+    for k in range(8):
+        dtab = dma("s" if k < 4 else "a", "dtab", T.tb[16 * k:16 * k + 16, :], T.cnt[:])
+    dx = dma("s", "dx", T.xt[:], T.x[:])
+    dw0 = dma("a", "dw0", T.wt[:, 0:1536], T.w[:, 0:1536])
+    dw1 = dma("s", "dw1", T.wt[:, 1536:3072], T.w[:, 1536:3072])
+
+    flag = {"allow_small_or_imprecise_dtypes": True}
+    k0 = do("g", (), lambda: g.iota(T.pi[:], [[0, 1]], 0, 1))
+    k1 = do("g", (), lambda: g.iota(T.c16[:], [[16, 16]], 0, 0, **flag))
+    k2 = do("g", (), lambda: g.iota(T.c1[:], [[1, 16]], 0, 0, **flag))
+    k3 = do("g", (), lambda: g.iota(T.ir[:, 0:C], [[1, C]], 0, 0, **flag))
+    k4 = do("g", (), lambda: g.iota(T.mi[:], [[0, 24], [1, 16]], 0, 15))
+    u = fill(T.T1[:], 0.0)
+    u = fill(T.rm[:], 1.0)
+    fr = do("v", [u], lambda: V.memset(T.rm[:, 0:32:16], 0.0))
+    fr = do("v", [u], lambda: V.memset(T.rm[:, 64:96:16], 0.0))
+    fill(T.cc[:], 0.0)
+    fill(T.cn[:], -1.0)
+    fill(T.er[:, 0:1], 0.0)
+    for k, v in enumerate([W0 - P * (r - 2), W0 - P * (r + 2), W0 - P * dest.get("z", 0), W0 - P * r, -P * dest.get("z", 0) - 0.5]):
+        fcb = fill(T.cb[:, k:k + 1], float(v))
+    fpw = fill(T.pw[:, W0 - 16:W0 + P], 0.0)
+    if r == 0:
+        tS = fill(T.S[:], 0.0)
+    u = ts([k0], T.pa[:], T.pi[:], 15, Op.bitwise_and)
+    u = tc([u], T.pf[:], T.pa[:])
+    j0 = ts([u, k1], T.tj[:], T.c16[:], T.pf[:], Op.add)
+    u = ts([u], T.p12[:], T.pf[:], 12.0, Op.mult)
+    c12 = ts([u, k2], T["ord"][:], T.c1[:, 0:12], T.p12[:], Op.add)
+    j1 = ts([j0], T.tj192[:], T.tj[:], float(C), Op.add)
+    j2 = ts([j0], T.tjtr[:], T.tj[:], float(TR), Op.add)
+    j3 = ts([j0], T.m2[:], T.tj[:], -2.0, Op.mult, -190.0, Op.add)
+    kr = ts([k3], T.kr[:, 0:C], T.ir[:, 0:C], float(C), Op.add)
+    ep = ts([k3], T.er[:, C:2 * C], T.ir[:, 0:C], float(TR), Op.add)
+    u = ts([k4], T.mj[:], T.mi[:], 15, Op.bitwise_and)
+    mk = ts([u], T.mask[:], T.mj[:], 0.0, Op.is_equal, BIG, Op.mult)
+    u = ts([k3], T.ir[:, C:2 * C], T.ir[:, 0:C], float(C), Op.add)
+    ir = ts([u], T.ir[:, 2 * C:WIN], T.ir[:, 0:WIN - 2 * C], 2.0 * C, Op.add)
+
+    pb = do("g", [drow], lambda: g.partition_broadcast(T.rowi[:], T.row1[0:1, :], 128))
+
+    a0 = tc([dtab], T.T1[:, 0:12], T.tb[:])
+    a1 = ts([dtab], T.T1[:, 64:76], T.tb[:], 0.0, Op.is_gt)
+    z0 = ts([dtab], T.z0[:], T.tb[:], 0.0, Op.is_equal)
+    b1 = do("v", [a1, fr], lambda: V.transpose(T.A1[:], T.T1[:]))
+    z1 = tt([z0, j1], T.z1[:], T.z0[:], T.tj192[:, 0:12], Op.mult)
+    b2 = scan([b1], T.B1[:], T.rm[:], T.A1[:], 0.0, Op.mult, Op.add)
+    z2 = tt([z0], T.z2[:], T.z0[:], T.tjtr[:, 0:12], Op.mult)
+    b3 = do("v", [b2], lambda: V.transpose(T.Z1[:], T.B1[:]))
+    tot = scan([b3], T.cc[:, 1:13], T.Z1[:, 32:44], T.Z1[:, 32:44], 0.0, Op.add, Op.max)
+    nn = scan([b3], T.cn[:, 1:13], T.Z1[:, 96:108], T.Z1[:, 96:108], -1.0, Op.add, Op.add) if False else \
+        do("v", [b3], lambda: V.tensor_tensor_scan(T.cn[:, 1:13], T.Z1[:, 96:108], T.T1[:, 12:24], -1.0, Op.add, Op.add))
+    hi = list(range(r + 1, N))
+    if hi:
+        fused([tot], [(hi, common(topo, core, [cores[d] for d in hi]), "atot", T.cc[:, 12:13], T.tl[:, r:r + 1])])
+
+    o = tt([nn], T.o1[:], T.Z1[:, 64:76], T.cn[:, 0:12], Op.add)
+    o = tt([o, z1], T.o2[:], T.o1[:], T.z1[:], Op.max)
+    o = tc([o], T.ok[:], T.o2[:])
+    ks = tc([o, kr], T.kr[:, 0:2 * C].indirect(T.ok[:, 0:12]), T.ir[:, 0:C])
+    qx = do("v", [dx], lambda: V.quantize_mx(T.raw[:, 0:C], T.raws[:, 0:C], T.xt[:, 0:4 * C]))
+    ma = me[r][0]
+    pe = topo.engines(core, cores[pt])
+    pa = seg(pt)[r][0]
+    fused([qx], [([pt], pe, "apc", T.raw[:, 0:C].bitcast(dt.uint8), T.win[:, pa:pa + C].bitcast(dt.uint8))])
+    fused([qx], [([pt], pe, "apc", T.raws[:, 0:C], T.wins[:, pa:pa + C])])
+    dma("s", "down", T.win[:, ma:ma + C].bitcast(dt.uint8), T.raw[:, 0:C].bitcast(dt.uint8), [qx])
+    down = dma("s", "down", T.wins[:, ma:ma + C], T.raws[:, 0:C], [qx])
+    kd = scan([ks, mk], T.kd[:], T.mask[:, 0:C], T.kr[:, 0:C], 0.0, Op.max, Op.min)
+    kl = ts([kd], T.kl[:], T.kd[:, 15:C:16], C - 1.0, Op.min)
+    ke = tc([kd], T.ke[:], T.kd[:, 15:C:16])
+    f2 = ts([nn], T.f2[:], T.cn[:, 12:13], H - 1.0, Op.subtract, 0.0, Op.max)
+    cq = pick([kl, qx], T.comp[:, 0:C], T.raw[:, 0:C], T.kl[:, 0:12])
+    cs = act([kl, qx], T.comps[:, 0:C], T.raws[:, 0:C].indirect(T.kl[:, 0:12]))
+    if "p2" in dest:
+        l2 = ts([f2], T.l2[:, 0:7], T.tj[:, 0:7], T.f2[:], Op.add)
+        q2 = pick([l2, cq], T.sel2[:, 0:H], T.comp[:, 0:C], T.l2[:, 0:7])
+
+    def land(d):
+        a, n = seg(d)[r]
+        return a, a + n
+
+    src = {"m2": (T.comp, T.comps, cq, cs)}
+    if "p2" in dest:
+        q2s = act([l2, cs], T.sel2s[:, 0:H], T.comps[:, 0:C].indirect(T.l2[:, 0:7]))
+        src["p2"] = (T.sel2, T.sel2s, q2, q2s)
+
+    def send_cols(kinds, scales):
+        m = masks(r, kinds)
+        trs, deps = [], []
+        for k in m:
+            a, b = land(dest[k])
+            if scales:
+                trs.append(([dest[k]], m[k], "acd", src[k][1][:, 0:H], T.wins[:, a:b]))
+                deps.append(src[k][3])
+            else:
+                trs.append(([dest[k]], m[k], "acd", src[k][0][:, 0:H].bitcast(dt.uint8), T.win[:, a:b].bitcast(dt.uint8)))
+                deps.append(src[k][2])
+        if trs:
+            fused(deps, trs)
+
+    send_cols(("m2", "p2"), False)
+
+    cr = tc([pb, c12], T.cr[:], T.rowi[:, 0:C].indirect(T["ord"][:, 0:12]))
+    er = scan([cr], T.er[:, 1:C], T.cr[:, 0:C - 1], T.cr[:, 0:C - 1], 0.0, Op.add, Op.max)
+    sc = act([er, ep, ke], T.sc[:], T.er[:, 0:2 * C].indirect(T.ke[:, 0:12]))
+    s1 = tt([tot], T.s1[:], T.Z1[:, 0:12], T.cc[:, 0:12], Op.add)
+    s1 = tt([s1], T.s2[:], T.s1[:], T.T1[:, 0:12], Op.subtract)
+    sx = tt([s1, z2], T.sx[:], T.s2[:], T.z2[:], Op.max)
+    sxu = tc([sx], T.sxu[:], T.sx[:])
+    fused([sxu], [([pt], pe, "apt", T.sxu[:], T.pt[:])])
+    drows = {}
+    if "m2" in dest:
+        drows["m2"] = (T.d0, T.t0, 0, scan([sc], T.d0[:], T.mask[:, 0:H], T.sc[:, 0:H], 0.0, Op.max, Op.min))
+    if "p2" in dest:
+        r2 = act([sc, l2], T.r2[:], T.sc[:, 0:C].indirect(T.l2[:, 0:7]))
+        drows["p2"] = (T.d2, T.t2, 1, scan([r2], T.d2[:], T.mask[:, 0:H], T.r2[:], 0.0, Op.max, Op.min))
+
+    if r > 0:
+        na = sum(len(common(topo, cores[s], [cores[d] for d in range(s + 1, N)])) for s in range(r))
+        tS = do("v", [("atot", na)], lambda: V.tensor_reduce(T.S[:], T.tl[:, 0:r], AxisListType.X, Op.add))
+    bc = ts([tS, fcb], T.bc[:, 0:5], T.cb[:, 0:5], T.S[:], Op.add)
+    if "z" in dest:
+        ac = act([bc, sc], T.jk[:], T.sc[:], Act.Sign, bias=T.bc[:, 4:5], accum_out=T.acc[:])
+    tabs = {}
+    for k in drows:
+        d, t, i, tok = drows[k]
+        tabs[k] = (t, ts([tok, bc], t[:, 0:7], d[:, 15:H:16], T.bc[:, i:i + 1], Op.add))
+    if "z" in dest:
+        u = ts([ac], T.fz[:], T.acc[:], 190.0, Op.min, 30.0, Op.max)
+        lz = ts([u, j3], T.lz[:, 0:7], T.m2[:, 0:7], T.fz[:], Op.add, -0.5, Op.mult)
+        rz = act([lz], T.rz[:], T.sc[:, 0:C].indirect(T.lz[:, 0:7]))
+        qzs = act([lz, cs], T.selzs[:, 0:H], T.comps[:, 0:C].indirect(T.lz[:, 0:7]))
+        qz = pick([lz, cq], T.selz[:, 0:H], T.comp[:, 0:C], T.lz[:, 0:7])
+        src["z"] = (T.selz, T.selzs, qz, qzs)
+        u = scan([rz], T.dz[:], T.mask[:, 0:H], T.rz[:], 0.0, Op.max, Op.min)
+        tabs["z"] = (T.tz, ts([u, bc], T.tz[:, 0:7], T.dz[:, 15:H:16], T.bc[:, 2:3], Op.add))
+    slot = {"m2": 0, "p2": 8, "z": 16}
+    m = masks(r, ("m2", "p2", "z"))
+    send_cols(("z",), False)
+    fused([tabs[k][1] for k in m], [([dest[k]], m[k], "act", tabs[k][0][:, 0:7], T.ct[:, slot[k]:slot[k] + 7]) for k in m])
+    send_cols(("m2", "p2", "z"), True)
+
+    qw0 = do("v", [dw0], lambda: V.quantize_mx(T.wq[:, 0:384], T.ws[:, 0:384], T.wt[:, 0:1536]))
+    qw1 = do("v", [dw1], lambda: V.quantize_mx(T.wq[:, 384:768], T.ws[:, 384:768], T.wt[:, 1536:3072]))
+
+    def put(deps, offs, s):
+        a, n = me[s]
+        return tc(deps, T.pw[:].indirect(offs), T.ir[:, a:a + n])
+
+    u = ts([bc, sx], T.oo[:], T.sx[:], T.bc[:, 3:4], Op.add)
+    pp = put([u, fpw, ir], T.oo[:, 0:12], r)
+    if pt > r:
+        u = tt([bc], T.pc[:], T.bc[:, 3:4], T.cc[:, 12:13], Op.add)
+    else:
+        u = tt([bc], T.pc[:], T.bc[:, 3:4], T.tl[:, pt:pt + 1], Op.subtract)
+    npe = len(topo.engines(cores[pt], core))
+    u = ts([u, ("apt", npe)], T.po[:], T.pt[:], T.pc[:], Op.add)
+    pp = put([u, pp], T.po[:, 0:12], pt)
+    back = {"m2": "p2", "p2": "m2", "z": "z"}
+    nct = sum(len(masks(s, ("m2", "p2", "z"))[back[k]]) for k, s in off(r))
+    for k, s in off(r):
+        pp = put([("act", nct), pp], T.ct[:, slot[back[k]]:slot[back[k]] + 7], s)
+    u = scan([pp], T.pm[:], T.pw[:, W0 - 16:W0 + P], T.pw[:, W0 - 16:W0 + P], 0.0, Op.max, Op.max)
+    u = scan([u], T.pd[:], T.mask[:], T.pm[:, 16:16 + P], 0.0, Op.max, Op.min)
+    il = tc([u], T.il[:], T.pd[:, 15:P:16])
+
+    ncd = 0
+    for k, s in off(r):
+        b = back[k]
+        ncd += len(masks(s, ("m2", "p2"))[b]) if b != "z" else len(masks(s, ("z",))[b])
+        ncd += len(masks(s, ("m2", "p2", "z"))[b])
+    got = [il, down, ("apc", 2 * npe), ("acd", ncd)]
+    picks = []
+    for b in range(NB):
+        i = slice(128 * b, 128 * b + 128)
+        o = T.il[:, 8 * b:8 * b + 8]
+        picks.append((pick(got, T.fin[:, i], T.win[:], o), act(got, T.fins[:, i], T.wins[:].indirect(o))))
+    for b in range(NB):
+        i = slice(128 * b, 128 * b + 128)
+        for h in range(NO):
+            k = NO * b + h
+            wi = slice(128 * k, 128 * k + 128)
+            mm = do("t", list(picks[b]) + [qw0, qw1], lambda: g.tensor.matmul_mx(
+                T.ps[:, 512 * k:512 * k + 128], T.wq[:, wi], T.ws[:, wi], T.fin[:, i], T.fins[:, i], True, True))
+            yi = slice(P * h + 128 * b, P * h + 128 * b + 128)
+            cp = tc([mm], T.ysb[:, yi], T.ps[:, 512 * k:512 * k + 128]) if h == 0 else act([mm], T.ysb[:, yi], T.ps[:, 512 * k:512 * k + 128])
+            dma("s", "dy", T.y[:, yi], T.ysb[:, yi], [cp])
+
+    need("s", [("dy", total["dy"])])
+    g.wait_ge(T.sem.sent, sent[0])
+    need("g", [(s, total[s]) for s in total if s != "dy"])

@@ -3,7 +3,7 @@ from concourse.mybir import dt, AluOpType as Op, AxisListType, ActivationFunctio
 
 C, P, NB, NO, H = 192, 384, 3, 2, 112
 W0 = 1536
-TR = 2048
+TR = 3584
 BIG = 1.0e6
 WIN = 3 * H + 2 * C
 F32, I32, U16, U8, F8, BF = "float32", "int32", "uint16", "uint8", "float8_e4m3fn_x4", "bfloat16"
@@ -20,21 +20,21 @@ SCRATCH = {
     "win": sb(WIN, F8), "wins": sb(WIN, U8), "fin": sb(P, F8), "fins": sb(P, U8),
     "pi": sb(1, I32), "pa": sb(1, I32), "pf": sb(1, F32), "p12": sb(1, F32), "c16": sb(16, F32), "c1": sb(16, F32),
     "tj": sb(16, F32), "tj192": sb(16, F32), "tjtr": sb(16, F32), "m2": sb(16, F32), "ord": sb(12, U16),
-    "ir": sb(WIN, F32), "mi": sb(P, I32), "mj": sb(P, I32), "mask": sb(P, F32), "rm": sb(128, F32), "cb": sb(8, F32),
+    "ir": sb(WIN, F32), "vz": sb(2 * H, F32), "mi": sb(16, I32), "mj": sb(16, I32), "mask": sb(P, F32), "rm": sb(128, F32),
     "tb": sb(12, I32), "row1": sb(C, I32), "rowi": sb(C, I32), "T1": sb(128, F32), "A1": sb(128, F32), "B1": sb(128, F32),
     "Z1": sb(128, F32), "cc": sb(16, F32), "cn": sb(16, F32), "z0": sb(12, F32), "z1": sb(12, F32), "z2": sb(12, F32),
     "o1": sb(12, F32), "o2": sb(12, F32), "ok": sb(12, U16), "kr": sb(2 * C, F32), "kd": sb(C, F32),
-    "kl": sb(12, U16), "ke": sb(12, U16), "cr": sb(C, F32), "er": sb(2 * C, F32), "sc": sb(C, F32),
+    "kl": sb(12, U16), "ke": sb(12, U16), "cr": sb(C, F32), "er": sb(2 * C, F32), "sc": sb(C + 128, F32),
     "s1": sb(12, F32), "s2": sb(12, F32), "sx": sb(12, F32), "sxu": sb(12, U16),
     "f2": sb(1, F32), "l2": sb(8, U16), "r2": sb(H, F32), "d0": sb(H, F32), "d2": sb(H, F32), "dz": sb(H, F32),
     "t0": sb(8, U16), "t2": sb(8, U16), "tz": sb(8, U16), "rz": sb(H, F32),
-    "tl": sb(8, F32), "S": sb(1, F32), "bc": sb(8, F32), "pc": sb(1, F32), "jk": sb(C, F32), "acc": sb(1, F32), "fz": sb(1, F32),
-    "lz": sb(8, U16), "pt": sb(12, U16), "po": sb(12, U16), "oo": sb(12, U16), "ct": sb(24, U16),
-    "pw": sb(6144, F32), "pm": sb(P + 16, F32), "pd": sb(P, F32), "il": sb(24, U16),
+    "tl": sb(16, F32), "S": sb(1, F32), "pc": sb(1, F32), "jk": sb(C, F32), "acc": sb(1, F32),
+    "lze": sb(8, U16), "lzc": sb(8, U16), "pt": sb(12, U16), "po": sb(24, U16), "ct": sb(16, U16), "cz": sb(8, U16),
+    "pw": sb(10752, F32), "pm": sb(P + 16, F32), "pd": sb(P, F32), "il": sb(24, U16),
     "ysb": sb(NO * P, F32), "ps": ("psum", [128, 512 * 6], F32),
 }
 SEMAPHORES = ["sv", "sa", "sg", "st", "dtab", "drow", "dx", "dw0", "dw1", "down", "dy", "sent",
-              "atot", "apt", "apc", "act", "acd"]
+              "atot", "apt", "apc", "act", "acz", "acd"]
 
 
 def common(topo, src, dsts):
@@ -42,15 +42,6 @@ def common(topo, src, dsts):
     for d in dsts[1:]:
         e = [k for k in e if k in topo.engines(src, d)]
     return e
-
-
-def groups(e, k):
-    n = len(e)
-    if k == 1:
-        return [e]
-    if k == 2:
-        return [e[:n // 2], e[n // 2:]]
-    return [e[:n // 4], e[n // 4:n // 2], e[n // 2:]]
 
 
 def bits(e):
@@ -70,28 +61,33 @@ def rank_program(g, core, T, topo):
     def partner(q):
         return [d for d in (q - 1, q + 1) if 0 <= d < N and topo.chip(cores[d]) == topo.chip(cores[q])][0]
 
-    def off(q):
-        v = [("m2", q - 2), ("p2", q + 2)] + [("z", d) for d in (q - 1, q + 1) if d != partner(q)]
-        return [(k, d) for k, d in v if 0 <= d < N]
+    def two(q):
+        return [d for d in (q - 2, q + 2) if 0 <= d < N]
+
+    def zed(q):
+        return [d for d in (q - 1, q + 1) if 0 <= d < N and d != partner(q)]
 
     def seg(d):
         a, o = {}, 0
-        for s in range(d - 2, d + 3):
-            if 0 <= s < N:
-                n = C if s in (d, partner(d)) else H
-                a[s] = (o, n)
-                o += n
+        for s in range(max(0, d - 2), min(N, d + 3)):
+            n = C if s in (d, partner(d)) else H
+            a[s] = (o, n)
+            o += n
         return a
 
-    def masks(q, kinds):
-        ks = [(k, d) for k, d in off(q) if k in kinds]
-        if not ks:
-            return {}
-        return dict(zip([k for k, d in ks], groups(common(topo, cores[q], [cores[d] for k, d in ks]), len(ks))))
+    def eng(q):
+        return common(topo, cores[q], [c for c in cores if c != cores[q]])
 
-    pt = partner(r)
-    me = seg(r)
-    dest = dict(off(r))
+    def share(q, d):
+        e, v = eng(q), two(q)
+        n = len(e) // len(v)
+        return e[n * v.index(d):n * v.index(d) + n]
+
+    pt, me, E = partner(r), seg(r), eng(r)
+    lo2 = r - 2 if r - 2 >= 0 else None
+    hi2 = r + 2 if r + 2 < N else None
+    z = (zed(r) + [None])[0]
+    tr = float(TR * (1 + (r + r // (N // 2)) % 2))
     qs = {"v": g.vector, "a": g.scalar, "s": g.sync, "t": g.tensor, "g": g}
     home = {"v": "sv", "a": "sa", "t": "st", "g": "sg"}
     seen, total = {}, {}
@@ -123,7 +119,7 @@ def rank_program(g, core, T, topo):
     def fused(deps, trs):
         need("g", deps)
         g.remote_dma_fused([RemoteDMATransfer(dst_ids=[dst(cores[d]) for d in ds], dma_engine_mask=bits(e), remote_sem=T.sem[sem],
-                                              srcs=[a], dsts=[b] * len(ds)) for ds, e, sem, a, b in trs], local_sem=T.sem.sent)
+                                              srcs=[a], dsts=b) for ds, e, sem, a, b in trs], local_sem=T.sem.sent)
         sent[0] += sum(len(e) for ds, e, sem, a, b in trs)
 
     def tc(deps, out, in_):
@@ -140,6 +136,9 @@ def rank_program(g, core, T, topo):
     def scan(deps, out, a, b, init, op0, op1):
         return do("v", deps, lambda: V.tensor_tensor_scan(out, a, b, init, op0, op1))
 
+    def diag(deps, out, row, n):
+        return scan(deps, out, T.mask[:, 0:n], row, 0.0, Op.max, Op.min)
+
     def fill(ap, c):
         return do("v", (), lambda: V.memset(ap, c))
 
@@ -149,185 +148,178 @@ def rank_program(g, core, T, topo):
     def pick(deps, out, in_, o):
         return tc(deps, out.bitcast(dt.uint32), in_.bitcast(dt.uint32).indirect(o))
 
-    drow = dma("s", "drow", T.row1[0:1, :], T.cnt[:])
+    def codes(ap):
+        return ap.bitcast(dt.uint8)
+
     for k in range(8):
         dtab = dma("s" if k < 4 else "a", "dtab", T.tb[16 * k:16 * k + 16, :], T.cnt[:])
-    dx = dma("s", "dx", T.xt[:], T.x[:])
-    dw0 = dma("a", "dw0", T.wt[:, 0:1536], T.w[:, 0:1536])
+    drow = dma("s", "drow", T.row1[0:1, :], T.cnt[:])
+    dx = dma("a", "dx", T.xt[:], T.x[:])
+    dw0 = dma("s", "dw0", T.wt[:, 0:1536], T.w[:, 0:1536])
     dw1 = dma("s", "dw1", T.wt[:, 1536:3072], T.w[:, 1536:3072])
 
     flag = {"allow_small_or_imprecise_dtypes": True}
     k0 = do("g", (), lambda: g.iota(T.pi[:], [[0, 1]], 0, 1))
     k1 = do("g", (), lambda: g.iota(T.c16[:], [[16, 16]], 0, 0, **flag))
     k2 = do("g", (), lambda: g.iota(T.c1[:], [[1, 16]], 0, 0, **flag))
+    k4 = do("g", (), lambda: g.iota(T.mi[:], [[1, 16]], 0, 15))
     k3 = do("g", (), lambda: g.iota(T.ir[:, 0:C], [[1, C]], 0, 0, **flag))
-    k4 = do("g", (), lambda: g.iota(T.mi[:], [[0, 24], [1, 16]], 0, 15))
-    u = fill(T.T1[:], 0.0)
+    ft = fill(T.T1[:], 0.0)
     u = fill(T.rm[:], 1.0)
-    fr = do("v", [u], lambda: V.memset(T.rm[:, 0:32:16], 0.0))
-    fr = do("v", [u], lambda: V.memset(T.rm[:, 64:96:16], 0.0))
     fill(T.cc[:], 0.0)
     fill(T.cn[:], -1.0)
+    fr = do("v", [u], lambda: V.memset(T.rm[:, 0:32:16], 0.0))
+    fr = do("v", [u], lambda: V.memset(T.rm[:, 64:96:16], 0.0))
+    shift = -P * z - 0.5 if z is not None else 0.0
+    fs = fill(T.tl[:, 8:9], shift)
     fill(T.er[:, 0:1], 0.0)
-    for k, v in enumerate([W0 - P * (r - 2), W0 - P * (r + 2), W0 - P * dest.get("z", 0), W0 - P * r, -P * dest.get("z", 0) - 0.5]):
-        fcb = fill(T.cb[:, k:k + 1], float(v))
-    fpw = fill(T.pw[:, W0 - 16:W0 + P], 0.0)
     if r == 0:
-        tS = fill(T.S[:], 0.0)
+        tS = fill(T.S[:], shift)
     u = ts([k0], T.pa[:], T.pi[:], 15, Op.bitwise_and)
+    v = ts([k4], T.mj[:], T.mi[:], 15, Op.bitwise_and)
     u = tc([u], T.pf[:], T.pa[:])
+    mk = ts([v], T.mask[:, 0:16], T.mj[:], 0.0, Op.is_equal, BIG, Op.mult)
     j0 = ts([u, k1], T.tj[:], T.c16[:], T.pf[:], Op.add)
     u = ts([u], T.p12[:], T.pf[:], 12.0, Op.mult)
-    c12 = ts([u, k2], T["ord"][:], T.c1[:, 0:12], T.p12[:], Op.add)
     j1 = ts([j0], T.tj192[:], T.tj[:], float(C), Op.add)
-    j2 = ts([j0], T.tjtr[:], T.tj[:], float(TR), Op.add)
-    j3 = ts([j0], T.m2[:], T.tj[:], -2.0, Op.mult, -190.0, Op.add)
-    kr = ts([k3], T.kr[:, 0:C], T.ir[:, 0:C], float(C), Op.add)
-    ep = ts([k3], T.er[:, C:2 * C], T.ir[:, 0:C], float(TR), Op.add)
-    u = ts([k4], T.mj[:], T.mi[:], 15, Op.bitwise_and)
-    mk = ts([u], T.mask[:], T.mj[:], 0.0, Op.is_equal, BIG, Op.mult)
-    u = ts([k3], T.ir[:, C:2 * C], T.ir[:, 0:C], float(C), Op.add)
-    ir = ts([u], T.ir[:, 2 * C:WIN], T.ir[:, 0:WIN - 2 * C], 2.0 * C, Op.add)
+    c12 = ts([u, k2], T["ord"][:], T.c1[:, 0:12], T.p12[:], Op.add)
+    j2 = ts([j0], T.tjtr[:], T.tj[:], tr, Op.add)
+    j3 = ts([j0], T.m2[:], T.tj[:], -2.0, Op.mult, -float(C), Op.add)
+    n = 16
+    while n < P:
+        w = min(n, P - n)
+        mk = act([mk], T.mask[:, n:n + w], T.mask[:, 0:w])
+        n += w
+        if n == 64:
+            kr = act([k3], T.kr[:, 0:C], T.ir[:, 0:C], Act.Identity, bias=float(C))
+        if n == 256:
+            ep = act([k3], T.er[:, C:2 * C], T.ir[:, 0:C], Act.Identity, bias=tr)
+            i1 = act([k3], T.ir[:, C:2 * C], T.ir[:, 0:C], Act.Identity, bias=float(C))
 
     pb = do("g", [drow], lambda: g.partition_broadcast(T.rowi[:], T.row1[0:1, :], 128))
 
+    a1 = ts([dtab, ft], T.T1[:, 64:76], T.tb[:], 0.0, Op.is_gt)
     a0 = tc([dtab], T.T1[:, 0:12], T.tb[:])
-    a1 = ts([dtab], T.T1[:, 64:76], T.tb[:], 0.0, Op.is_gt)
     z0 = ts([dtab], T.z0[:], T.tb[:], 0.0, Op.is_equal)
-    b1 = do("v", [a1, fr], lambda: V.transpose(T.A1[:], T.T1[:]))
+    b1 = do("v", [a0, fr], lambda: V.transpose(T.A1[:], T.T1[:]))
     z1 = tt([z0, j1], T.z1[:], T.z0[:], T.tj192[:, 0:12], Op.mult)
     b2 = scan([b1], T.B1[:], T.rm[:], T.A1[:], 0.0, Op.mult, Op.add)
-    z2 = tt([z0], T.z2[:], T.z0[:], T.tjtr[:, 0:12], Op.mult)
+    z2 = tt([z0, j2], T.z2[:], T.z0[:], T.tjtr[:, 0:12], Op.mult)
     b3 = do("v", [b2], lambda: V.transpose(T.Z1[:], T.B1[:]))
-    tot = scan([b3], T.cc[:, 1:13], T.Z1[:, 32:44], T.Z1[:, 32:44], 0.0, Op.add, Op.max)
-    nn = scan([b3], T.cn[:, 1:13], T.Z1[:, 96:108], T.Z1[:, 96:108], -1.0, Op.add, Op.add) if False else \
-        do("v", [b3], lambda: V.tensor_tensor_scan(T.cn[:, 1:13], T.Z1[:, 96:108], T.T1[:, 12:24], -1.0, Op.add, Op.add))
+    nn = scan([b3], T.cn[:, 1:13], T.Z1[:, 96:108], T.T1[:, 12:24], -1.0, Op.add, Op.add)
+    tot = scan([b3], T.cc[:, 1:13], T.Z1[:, 32:44], T.T1[:, 12:24], 0.0, Op.add, Op.add)
     hi = list(range(r + 1, N))
     if hi:
-        fused([tot], [(hi, common(topo, core, [cores[d] for d in hi]), "atot", T.cc[:, 12:13], T.tl[:, r:r + 1])])
-
+        fused([tot], [(hi, E, "atot", T.cc[:, 12:13], [T.tl[:, 8 - d + r:9 - d + r] for d in hi])])
     o = tt([nn], T.o1[:], T.Z1[:, 64:76], T.cn[:, 0:12], Op.add)
+    s1 = tt([tot], T.s1[:], T.Z1[:, 0:12], T.cc[:, 0:12], Op.add)
     o = tt([o, z1], T.o2[:], T.o1[:], T.z1[:], Op.max)
+    s1 = tt([s1], T.s2[:], T.s1[:], T.T1[:, 0:12], Op.subtract)
     o = tc([o], T.ok[:], T.o2[:])
-    ks = tc([o, kr], T.kr[:, 0:2 * C].indirect(T.ok[:, 0:12]), T.ir[:, 0:C])
     qx = do("v", [dx], lambda: V.quantize_mx(T.raw[:, 0:C], T.raws[:, 0:C], T.xt[:, 0:4 * C]))
-    ma = me[r][0]
-    pe = topo.engines(core, cores[pt])
-    pa = seg(pt)[r][0]
-    fused([qx], [([pt], pe, "apc", T.raw[:, 0:C].bitcast(dt.uint8), T.win[:, pa:pa + C].bitcast(dt.uint8))])
-    fused([qx], [([pt], pe, "apc", T.raws[:, 0:C], T.wins[:, pa:pa + C])])
-    dma("s", "down", T.win[:, ma:ma + C].bitcast(dt.uint8), T.raw[:, 0:C].bitcast(dt.uint8), [qx])
-    down = dma("s", "down", T.wins[:, ma:ma + C], T.raws[:, 0:C], [qx])
-    kd = scan([ks, mk], T.kd[:], T.mask[:, 0:C], T.kr[:, 0:C], 0.0, Op.max, Op.min)
+    ks = tc([o, kr], T.kr[:, 0:2 * C].indirect(T.ok[:, 0:12]), T.ir[:, 0:C])
+    sx = tt([s1, z2], T.sx[:], T.s2[:], T.z2[:], Op.max)
+    f2 = ts([nn], T.f2[:], T.cn[:, 12:13], H - 1.0, Op.subtract, 0.0, Op.max)
+    kd = diag([ks, mk], T.kd[:], T.kr[:, 0:C], C)
+    sxu = tc([sx], T.sxu[:], T.sx[:])
+    if hi2 is not None:
+        l2 = ts([f2, j0], T.l2[:, 0:7], T.tj[:, 0:7], T.f2[:], Op.add)
     kl = ts([kd], T.kl[:], T.kd[:, 15:C:16], C - 1.0, Op.min)
     ke = tc([kd], T.ke[:], T.kd[:, 15:C:16])
-    f2 = ts([nn], T.f2[:], T.cn[:, 12:13], H - 1.0, Op.subtract, 0.0, Op.max)
     cq = pick([kl, qx], T.comp[:, 0:C], T.raw[:, 0:C], T.kl[:, 0:12])
-    cs = act([kl, qx], T.comps[:, 0:C], T.raws[:, 0:C].indirect(T.kl[:, 0:12]))
-    if "p2" in dest:
-        l2 = ts([f2], T.l2[:, 0:7], T.tj[:, 0:7], T.f2[:], Op.add)
-        q2 = pick([l2, cq], T.sel2[:, 0:H], T.comp[:, 0:C], T.l2[:, 0:7])
-
-    def land(d):
-        a, n = seg(d)[r]
-        return a, a + n
-
-    src = {"m2": (T.comp, T.comps, cq, cs)}
-    if "p2" in dest:
-        q2s = act([l2, cs], T.sel2s[:, 0:H], T.comps[:, 0:C].indirect(T.l2[:, 0:7]))
-        src["p2"] = (T.sel2, T.sel2s, q2, q2s)
-
-    def send_cols(kinds, scales):
-        m = masks(r, kinds)
-        trs, deps = [], []
-        for k in m:
-            a, b = land(dest[k])
-            if scales:
-                trs.append(([dest[k]], m[k], "acd", src[k][1][:, 0:H], T.wins[:, a:b]))
-                deps.append(src[k][3])
-            else:
-                trs.append(([dest[k]], m[k], "acd", src[k][0][:, 0:H].bitcast(dt.uint8), T.win[:, a:b].bitcast(dt.uint8)))
-                deps.append(src[k][2])
-        if trs:
-            fused(deps, trs)
-
-    send_cols(("m2", "p2"), False)
-
     cr = tc([pb, c12], T.cr[:], T.rowi[:, 0:C].indirect(T["ord"][:, 0:12]))
+    if hi2 is not None:
+        q2 = pick([l2, cq], T.sel2[:, 0:H], T.comp[:, 0:C], T.l2[:, 0:7])
     er = scan([cr], T.er[:, 1:C], T.cr[:, 0:C - 1], T.cr[:, 0:C - 1], 0.0, Op.add, Op.max)
-    sc = act([er, ep, ke], T.sc[:], T.er[:, 0:2 * C].indirect(T.ke[:, 0:12]))
-    s1 = tt([tot], T.s1[:], T.Z1[:, 0:12], T.cc[:, 0:12], Op.add)
-    s1 = tt([s1], T.s2[:], T.s1[:], T.T1[:, 0:12], Op.subtract)
-    sx = tt([s1, z2], T.sx[:], T.s2[:], T.z2[:], Op.max)
-    sxu = tc([sx], T.sxu[:], T.sx[:])
-    fused([sxu], [([pt], pe, "apt", T.sxu[:], T.pt[:])])
-    drows = {}
-    if "m2" in dest:
-        drows["m2"] = (T.d0, T.t0, 0, scan([sc], T.d0[:], T.mask[:, 0:H], T.sc[:, 0:H], 0.0, Op.max, Op.min))
-    if "p2" in dest:
-        r2 = act([sc, l2], T.r2[:], T.sc[:, 0:C].indirect(T.l2[:, 0:7]))
-        drows["p2"] = (T.d2, T.t2, 1, scan([r2], T.d2[:], T.mask[:, 0:H], T.r2[:], 0.0, Op.max, Op.min))
-
-    if r > 0:
-        na = sum(len(common(topo, cores[s], [cores[d] for d in range(s + 1, N)])) for s in range(r))
-        tS = do("v", [("atot", na)], lambda: V.tensor_reduce(T.S[:], T.tl[:, 0:r], AxisListType.X, Op.add))
-    bc = ts([tS, fcb], T.bc[:, 0:5], T.cb[:, 0:5], T.S[:], Op.add)
-    if "z" in dest:
-        ac = act([bc, sc], T.jk[:], T.sc[:], Act.Sign, bias=T.bc[:, 4:5], accum_out=T.acc[:])
-    tabs = {}
-    for k in drows:
-        d, t, i, tok = drows[k]
-        tabs[k] = (t, ts([tok, bc], t[:, 0:7], d[:, 15:H:16], T.bc[:, i:i + 1], Op.add))
-    if "z" in dest:
-        u = ts([ac], T.fz[:], T.acc[:], 190.0, Op.min, 30.0, Op.max)
-        lz = ts([u, j3], T.lz[:, 0:7], T.m2[:, 0:7], T.fz[:], Op.add, -0.5, Op.mult)
-        rz = act([lz], T.rz[:], T.sc[:, 0:C].indirect(T.lz[:, 0:7]))
-        qzs = act([lz, cs], T.selzs[:, 0:H], T.comps[:, 0:C].indirect(T.lz[:, 0:7]))
-        qz = pick([lz, cq], T.selz[:, 0:H], T.comp[:, 0:C], T.lz[:, 0:7])
-        src["z"] = (T.selz, T.selzs, qz, qzs)
-        u = scan([rz], T.dz[:], T.mask[:, 0:H], T.rz[:], 0.0, Op.max, Op.min)
-        tabs["z"] = (T.tz, ts([u, bc], T.tz[:, 0:7], T.dz[:, 15:H:16], T.bc[:, 2:3], Op.add))
-    slot = {"m2": 0, "p2": 8, "z": 16}
-    m = masks(r, ("m2", "p2", "z"))
-    send_cols(("z",), False)
-    fused([tabs[k][1] for k in m], [([dest[k]], m[k], "act", tabs[k][0][:, 0:7], T.ct[:, slot[k]:slot[k] + 7]) for k in m])
-    send_cols(("m2", "p2", "z"), True)
-
     qw0 = do("v", [dw0], lambda: V.quantize_mx(T.wq[:, 0:384], T.ws[:, 0:384], T.wt[:, 0:1536]))
-    qw1 = do("v", [dw1], lambda: V.quantize_mx(T.wq[:, 384:768], T.ws[:, 384:768], T.wt[:, 1536:3072]))
+    cs = act([kl, qx], T.comps[:, 0:C], T.raws[:, 0:C].indirect(T.kl[:, 0:12]))
+    sp = act([k3], T.sc[:, C:C + 128], T.ir[:, 0:128], Act.Identity, bias=tr + C)
+    sc = act([er, ep, ke], T.sc[:, 0:C], T.er[:, 0:2 * C].indirect(T.ke[:, 0:12]))
+    if hi2 is not None:
+        q2s = act([l2, cs], T.sel2s[:, 0:H], T.comps[:, 0:C].indirect(T.l2[:, 0:7]))
+        r2 = act([sc, l2], T.r2[:], T.sc[:, 0:C].indirect(T.l2[:, 0:7]))
 
-    def put(deps, offs, s):
-        a, n = me[s]
-        return tc(deps, T.pw[:].indirect(offs), T.ir[:, a:a + n])
+    ma, pa = me[r][0], seg(pt)[r][0]
+    fused([qx], [([pt], E, "apc", codes(T.raw[:, 0:C]), [codes(T.win[:, pa:pa + C])])])
+    fused([qx], [([pt], E, "apc", T.raws[:, 0:C], [T.wins[:, pa:pa + C]])])
+    dma("s", "down", codes(T.win[:, ma:ma + C]), codes(T.raw[:, 0:C]), [qx])
+    down = dma("s", "down", T.wins[:, ma:ma + C], T.raws[:, 0:C], [qx])
+    src = {}
+    if lo2 is not None:
+        src[lo2] = (T.comp, T.comps, cq, cs)
+    if hi2 is not None:
+        src[hi2] = (T.sel2, T.sel2s, q2, q2s)
+    at = {d: seg(d)[r][0] for d in seg(r)}
+    fused([src[d][2] for d in src], [([d], share(r, d), "acd", codes(src[d][0][:, 0:H]), [codes(T.win[:, at[d]:at[d] + H])]) for d in src])
+    fused([sxu], [([pt], E, "apt", T.sxu[:], [T.pt[:]])])
+    fused([src[d][3] for d in src], [([d], share(r, d), "acd", src[d][1][:, 0:H], [T.wins[:, at[d]:at[d] + H]]) for d in src])
 
-    u = ts([bc, sx], T.oo[:], T.sx[:], T.bc[:, 3:4], Op.add)
-    pp = put([u, fpw, ir], T.oo[:, 0:12], r)
+    tabs = {}
+    if lo2 is not None:
+        tabs[lo2] = (T.t0, T.d0, diag([sc], T.d0[:], T.sc[:, 0:H], H))
+    if hi2 is not None:
+        tabs[hi2] = (T.t2, T.d2, diag([r2], T.d2[:], T.r2[:], H))
+    if r > 0:
+        na = sum(len(eng(s)) for s in range(r))
+        tS = do("v", [("atot", na), fs], lambda: V.tensor_reduce(T.S[:], T.tl[:, 8 - r:9], AxisListType.X, Op.add))
+    if z is not None:
+        ac = act([tS, sc, sp], T.jk[:], T.sc[:, 1:C + 1], Act.Sign, bias=T.S[:], accum_out=T.acc[:])
+
+    def base(d):
+        return float(W0 - P * d) - shift
+
+    tk = {}
+    for d in tabs:
+        t, dd, tok = tabs[d]
+        tk[d] = ts([tok, tS], t[:, 0:7], dd[:, 15:H:16], T.S[:], Op.add, base(d), Op.add)
+    fused([tk[d] for d in tk], [([d], share(r, d), "act", tabs[d][0][:, 0:7], [T.ct[:, 7 * two(d).index(r):7 * two(d).index(r) + 7]]) for d in tk])
+    oa, ob = (0, 12) if pt > r else (12, 0)
+    oo = ts([tS, sx], T.po[:, oa:oa + 12], T.sx[:], T.S[:], Op.add, base(r), Op.add)
     if pt > r:
-        u = tt([bc], T.pc[:], T.bc[:, 3:4], T.cc[:, 12:13], Op.add)
+        pc = tt([tS], T.pc[:], T.S[:], T.cc[:, 12:13], Op.add)
     else:
-        u = tt([bc], T.pc[:], T.bc[:, 3:4], T.tl[:, pt:pt + 1], Op.subtract)
-    npe = len(topo.engines(cores[pt], core))
-    u = ts([u, ("apt", npe)], T.po[:], T.pt[:], T.pc[:], Op.add)
-    pp = put([u, pp], T.po[:, 0:12], pt)
-    back = {"m2": "p2", "p2": "m2", "z": "z"}
-    nct = sum(len(masks(s, ("m2", "p2", "z"))[back[k]]) for k, s in off(r))
-    for k, s in off(r):
-        pp = put([("act", nct), pp], T.ct[:, slot[back[k]]:slot[back[k]] + 7], s)
-    u = scan([pp], T.pm[:], T.pw[:, W0 - 16:W0 + P], T.pw[:, W0 - 16:W0 + P], 0.0, Op.max, Op.max)
-    u = scan([u], T.pd[:], T.mask[:], T.pm[:, 16:16 + P], 0.0, Op.max, Op.min)
-    il = tc([u], T.il[:], T.pd[:, 15:P:16])
+        pc = tt([tS], T.pc[:], T.S[:], T.tl[:, 7:8], Op.subtract)
+    qw1 = do("v", [dw1], lambda: V.quantize_mx(T.wq[:, 384:768], T.ws[:, 384:768], T.wt[:, 1536:3072]))
+    if z is not None:
+        le = ts([ac, j3], T.lze[:, 0:7], T.m2[:, 0:7], T.acc[:], Op.add, -0.5, Op.mult)
+        rz = act([le], T.rz[:], T.sc[:, 0:C + 128].indirect(T.lze[:, 0:7]))
+        lc = ts([le], T.lzc[:, 0:7], T.lze[:, 0:7], C - 1.0, Op.min)
+        qzs = act([lc, cs], T.selzs[:, 0:H], T.comps[:, 0:C].indirect(T.lzc[:, 0:7]))
+        qz = pick([lc, cq], T.selz[:, 0:H], T.comp[:, 0:C], T.lzc[:, 0:7])
+        u = diag([rz], T.dz[:], T.rz[:], H)
+        tz = ts([u], T.tz[:, 0:7], T.dz[:, 15:H:16], T.S[:], Op.add, base(z), Op.add)
+        fused([qz], [([z], E, "acd", codes(T.selz[:, 0:H]), [codes(T.win[:, at[z]:at[z] + H])])])
+        fused([tz], [([z], E, "acz", T.tz[:, 0:7], [T.cz[:, 0:7]])])
+        fused([qzs], [([z], E, "acd", T.selzs[:, 0:H], [T.wins[:, at[z]:at[z] + H]])])
 
-    ncd = 0
-    for k, s in off(r):
-        b = back[k]
-        ncd += len(masks(s, ("m2", "p2"))[b]) if b != "z" else len(masks(s, ("z",))[b])
-        ncd += len(masks(s, ("m2", "p2", "z"))[b])
-    got = [il, down, ("apc", 2 * npe), ("acd", ncd)]
+    act([i1], T.pw[:, W0 - 16:W0 + P - 16], T.ir[:, 0:P], scale=0.0)
+    fp = act([i1], T.pw[:, W0 + P - 16:W0 + P], T.ir[:, 0:16], scale=0.0)
+    ir = act([i1], T.ir[:, 2 * C:WIN], T.ir[:, 0:WIN - 2 * C], Act.Identity, bias=2.0 * C)
+    for k, s in enumerate(two(r)):
+        vz = act([ir], T.vz[:, H * k:H * k + H], T.ir[:, me[s][0]:me[s][0] + H])
+    po = ts([pc, ("apt", len(eng(pt)))], T.po[:, ob:ob + 12], T.pt[:], T.pc[:], Op.add, base(r), Op.add)
+    a = min(me[r][0], me[pt][0])
+    pp = tc([oo, po, fp, ir], T.pw[:].indirect(T.po[:, 0:24]), T.ir[:, a:a + 2 * C])
+    nt = len(two(r))
+    pp = tc([pp, vz, ("act", sum(len(share(s, r)) for s in two(r)))], T.pw[:].indirect(T.ct[:, 0:7 * nt]), T.vz[:, 0:H * nt])
+    if z is not None:
+        pp = tc([pp, ("acz", len(eng(z)))], T.pw[:].indirect(T.cz[:, 0:7]), T.ir[:, me[z][0]:me[z][0] + H])
+    h = 128 + 16
+    u = scan([pp], T.pm[:, 0:h], T.pw[:, W0 - 16:W0 + 128], T.pw[:, W0 - 16:W0 + 128], 0.0, Op.max, Op.max)
+    v = scan([u], T.pm[:, h:P + 16], T.pw[:, W0 + 128:W0 + P], T.pw[:, W0 + 128:W0 + P], T.pm[:, h - 1:h], Op.max, Op.max)
+    u = diag([u], T.pd[:, 0:128], T.pm[:, 16:h], 128)
+    v = diag([v], T.pd[:, 128:P], T.pm[:, h:P + 16], P - 128)
+    u = tc([u], T.il[:, 0:8], T.pd[:, 15:128:16])
+    v = tc([v], T.il[:, 8:24], T.pd[:, 143:P:16])
+
+    ncd = sum(2 * len(share(s, r)) for s in two(r)) + (2 * len(eng(z)) if z is not None else 0)
+    got = [down, ("apc", 2 * len(eng(pt))), ("acd", ncd)]
     picks = []
     for b in range(NB):
         i = slice(128 * b, 128 * b + 128)
         o = T.il[:, 8 * b:8 * b + 8]
-        picks.append((pick(got, T.fin[:, i], T.win[:], o), act(got, T.fins[:, i], T.wins[:].indirect(o))))
+        l = [v if b else u] + got
+        picks.append((pick(l, T.fin[:, i], T.win[:], o), act(l, T.fins[:, i], T.wins[:].indirect(o))))
     for b in range(NB):
         i = slice(128 * b, 128 * b + 128)
         for h in range(NO):

@@ -4,6 +4,7 @@ from concourse.mybir import dt, AluOpType as Op, AxisListType, ActivationFunctio
 C, P, NB, NO, H = 192, 384, 3, 2, 112
 W0 = 1536
 TR = 3584
+FAR = 4096
 BIG = 1.0e6
 WIN = 3 * H + 2 * C
 F32, I32, U16, U8, F8, BF = "float32", "int32", "uint16", "uint8", "float8_e4m3fn_x4", "bfloat16"
@@ -18,19 +19,18 @@ SCRATCH = {
     "raw": sb(C, F8), "raws": sb(C, U8), "comp": sb(C, F8), "comps": sb(C, U8),
     "sel2": sb(H, F8), "sel2s": sb(H, U8), "selz": sb(H, F8), "selzs": sb(H, U8),
     "win": sb(WIN, F8), "wins": sb(WIN, U8), "fin": sb(P, F8), "fins": sb(P, U8),
-    "pi": sb(1, I32), "pa": sb(1, I32), "pf": sb(1, F32), "p12": sb(1, F32), "c16": sb(16, F32), "c1": sb(16, F32),
-    "tj": sb(16, F32), "tj192": sb(16, F32), "tjtr": sb(16, F32), "m2": sb(16, F32), "ord": sb(12, U16),
-    "ir": sb(WIN, F32), "vz": sb(2 * H, F32), "mi": sb(16, I32), "mj": sb(16, I32), "mask": sb(P, F32), "rm": sb(128, F32),
-    "tb": sb(12, I32), "row1": sb(C, I32), "rowi": sb(C, I32), "T1": sb(128, F32), "A1": sb(128, F32), "B1": sb(128, F32),
-    "Z1": sb(128, F32), "cc": sb(16, F32), "cn": sb(16, F32), "z0": sb(12, F32), "z1": sb(12, F32), "z2": sb(12, F32),
-    "o1": sb(12, F32), "o2": sb(12, F32), "ok": sb(12, U16), "kr": sb(2 * C, F32), "kd": sb(C, F32),
-    "kl": sb(12, U16), "ke": sb(12, U16), "cr": sb(C, F32), "er": sb(2 * C, F32), "sc": sb(C + 128, F32),
-    "s1": sb(12, F32), "s2": sb(12, F32), "sx": sb(12, F32), "sxu": sb(12, U16),
+    "pi": sb(1, I32), "pa": sb(1, I32), "pf": sb(1, F32), "c16": sb(16, F32), "tj": sb(16, F32), "tji": sb(26, I32),
+    "tjj": sb(26, I32), "m2": sb(16, F32), "ir": sb(WIN, F32), "vz": sb(2 * H, F32), "mi": sb(16, I32), "mj": sb(16, I32),
+    "mask": sb(P, F32), "rm": sb(64, BF), "rs": sb(26, F32),
+    "tb": sb(12, I32), "row1": sb(C, BF), "row": sb(C, BF), "T1": sb(64, BF), "A1": sb(96, BF), "B1": sb(64, BF),
+    "Z1": sb(64, BF), "ee": sb(27, F32), "uu": sb(26, F32), "z0": sb(26, F32), "zz": sb(26, F32),
+    "sx": sb(26, F32), "su": sb(26, U16), "kr": sb(7680, F32), "kd": sb(C, F32), "kl": sb(12, U16), "ke": sb(12, U16),
+    "er": sb(2 * C, F32), "sc": sb(C, F32),
     "f2": sb(1, F32), "l2": sb(8, U16), "r2": sb(H, F32), "d0": sb(H, F32), "d2": sb(H, F32), "dz": sb(H, F32),
     "t0": sb(8, U16), "t2": sb(8, U16), "tz": sb(8, U16), "rz": sb(H, F32),
-    "tl": sb(16, F32), "S": sb(1, F32), "pc": sb(1, F32), "jk": sb(C, F32), "acc": sb(1, F32),
-    "lze": sb(8, U16), "lzc": sb(8, U16), "pt": sb(12, U16), "po": sb(24, U16), "ct": sb(16, U16), "cz": sb(8, U16),
-    "pw": sb(10752, F32), "pm": sb(P + 16, F32), "pd": sb(P, F32), "il": sb(24, U16),
+    "tl": sb(12, F32), "S": sb(1, F32), "pc": sb(1, F32), "jk": sb(C, F32), "js": sb(8, F32), "acc": sb(1, F32),
+    "lze": sb(8, U16), "pt": sb(12, U16), "po": sb(24, U16), "ct": sb(16, U16), "cz": sb(8, U16),
+    "pw": sb(11264, F32), "pm": sb(P + 16, F32), "pd": sb(P, F32), "il": sb(24, U16),
     "ysb": sb(NO * P, F32), "ps": ("psum", [128, 512 * 6], F32),
 }
 SEMAPHORES = ["sv", "sa", "sg", "st", "dtab", "drow", "dx", "dw0", "dw1", "down", "dy", "sent",
@@ -57,6 +57,7 @@ def rank_program(g, core, T, topo):
         return
     cores = T.cores
     N = len(cores)
+    half = N // 2
 
     def partner(q):
         return [d for d in (q - 1, q + 1) if 0 <= d < N and topo.chip(cores[d]) == topo.chip(cores[q])][0]
@@ -83,11 +84,19 @@ def rank_program(g, core, T, topo):
         n = len(e) // len(v)
         return e[n * v.index(d):n * v.index(d) + n]
 
+    def summed(d):
+        return list(range(d)) if d < half else list(range(d + 1, N))
+
+    def slot(s, d):
+        if s in summed(d):
+            return half - len(summed(d)) + summed(d).index(s)
+        return 2 * half if s == partner(d) and s < d else None
+
     pt, me, E = partner(r), seg(r), eng(r)
     lo2 = r - 2 if r - 2 >= 0 else None
     hi2 = r + 2 if r + 2 < N else None
     z = (zed(r) + [None])[0]
-    tr = float(TR * (1 + (r + r // (N // 2)) % 2))
+    tr = float(TR * (1 + (r + r // half) % 2))
     qs = {"v": g.vector, "a": g.scalar, "s": g.sync, "t": g.tensor, "g": g}
     home = {"v": "sv", "a": "sa", "t": "st", "g": "sg"}
     seen, total = {}, {}
@@ -152,184 +161,210 @@ def rank_program(g, core, T, topo):
         return ap.bitcast(dt.uint8)
 
     for k in range(8):
-        dtab = dma("s" if k < 4 else "a", "dtab", T.tb[16 * k:16 * k + 16, :], T.cnt[:])
-    drow = dma("s", "drow", T.row1[0:1, :], T.cnt[:])
+        dtab = dma("s" if k % 2 == 0 else "a", "dtab", T.tb[16 * k:16 * k + 16, :], T.cnt[:])
     dx = dma("a", "dx", T.xt[:], T.x[:])
-    dw0 = dma("s", "dw0", T.wt[:, 0:1536], T.w[:, 0:1536])
-    dw1 = dma("s", "dw1", T.wt[:, 1536:3072], T.w[:, 1536:3072])
 
     flag = {"allow_small_or_imprecise_dtypes": True}
-    k0 = do("g", (), lambda: g.iota(T.pi[:], [[0, 1]], 0, 1))
-    k1 = do("g", (), lambda: g.iota(T.c16[:], [[16, 16]], 0, 0, **flag))
-    k2 = do("g", (), lambda: g.iota(T.c1[:], [[1, 16]], 0, 0, **flag))
     k4 = do("g", (), lambda: g.iota(T.mi[:], [[1, 16]], 0, 15))
+    k1 = do("g", (), lambda: g.iota(T.c16[:], [[16, 16]], 0, 0, **flag))
+    k0 = do("g", (), lambda: g.iota(T.pi[:], [[0, 1]], 0, 1))
+    k5 = do("g", (), lambda: g.iota(T.tji[:], [[128, 26]], FAR, 1))
     k3 = do("g", (), lambda: g.iota(T.ir[:, 0:C], [[1, C]], 0, 0, **flag))
     ft = fill(T.T1[:], 0.0)
     u = fill(T.rm[:], 1.0)
-    fill(T.cc[:], 0.0)
-    fill(T.cn[:], -1.0)
-    fr = do("v", [u], lambda: V.memset(T.rm[:, 0:32:16], 0.0))
-    fr = do("v", [u], lambda: V.memset(T.rm[:, 64:96:16], 0.0))
-    shift = -P * z - 0.5 if z is not None else 0.0
-    fs = fill(T.tl[:, 8:9], shift)
-    fill(T.er[:, 0:1], 0.0)
-    if r == 0:
-        tS = fill(T.S[:], shift)
-    u = ts([k0], T.pa[:], T.pi[:], 15, Op.bitwise_and)
     v = ts([k4], T.mj[:], T.mi[:], 15, Op.bitwise_and)
-    u = tc([u], T.pf[:], T.pa[:])
+    fill(T.A1[:, 31:32], 0.0)
     mk = ts([v], T.mask[:, 0:16], T.mj[:], 0.0, Op.is_equal, BIG, Op.mult)
-    j0 = ts([u, k1], T.tj[:], T.c16[:], T.pf[:], Op.add)
-    u = ts([u], T.p12[:], T.pf[:], 12.0, Op.mult)
-    j1 = ts([j0], T.tj192[:], T.tj[:], float(C), Op.add)
-    c12 = ts([u, k2], T["ord"][:], T.c1[:, 0:12], T.p12[:], Op.add)
-    j2 = ts([j0], T.tjtr[:], T.tj[:], tr, Op.add)
-    j3 = ts([j0], T.m2[:], T.tj[:], -2.0, Op.mult, -float(C), Op.add)
+    fr = do("v", [u], lambda: V.memset(T.rm[:, 0:32:16], 0.0))
+    u = ts([k0], T.pa[:], T.pi[:], 15, Op.bitwise_and)
+    jj = ts([k5], T.tjj[:], T.tji[:], 16383 - 127 + 15, Op.bitwise_and)
+    pf = tc([u], T.pf[:], T.pa[:])
+
+    def const(deps, out, c):
+        return act([k1] + list(deps), out, T.c16[:, 0:1], Act.Identity, scale=0.0, bias=float(c))
+
+    shift = -P * z - 0.5 if z is not None else 0.0
+    fs = const((), T.tl[:, half:half + 1], shift if r < half else -(N * P + shift))
+    e0 = const((), T.er[:, 0:1], 0)
+    fz = const((), T.ee[:, 0:1], 0)
+    act([k1], T.rs[:, 0:13], T.c16[:, 0:13], Act.Identity, scale=0.0, bias=1.0)
+    act([k1], T.rs[:, 14:26], T.c16[:, 0:12], Act.Identity, scale=0.0, bias=1.0)
+    fz = const((), T.rs[:, 13:14], 0)
     n = 16
     while n < P:
         w = min(n, P - n)
         mk = act([mk], T.mask[:, n:n + w], T.mask[:, 0:w])
         n += w
+        if n == 32:
+            j0 = act([pf], T.tj[:], T.c16[:], Act.Identity, bias=T.pf[:])
         if n == 64:
             kr = act([k3], T.kr[:, 0:C], T.ir[:, 0:C], Act.Identity, bias=float(C))
+            j3 = act([j0], T.m2[:], T.tj[:], Act.Identity, scale=-2.0, bias=-float(C - H))
         if n == 256:
             ep = act([k3], T.er[:, C:2 * C], T.ir[:, 0:C], Act.Identity, bias=tr)
-            i1 = act([k3], T.ir[:, C:2 * C], T.ir[:, 0:C], Act.Identity, bias=float(C))
 
-    pb = do("g", [drow], lambda: g.partition_broadcast(T.rowi[:], T.row1[0:1, :], 128))
-
-    a1 = ts([dtab, ft], T.T1[:, 64:76], T.tb[:], 0.0, Op.is_gt)
-    a0 = tc([dtab], T.T1[:, 0:12], T.tb[:])
-    z0 = ts([dtab], T.z0[:], T.tb[:], 0.0, Op.is_equal)
-    b1 = do("v", [a0, fr], lambda: V.transpose(T.A1[:], T.T1[:]))
-    z1 = tt([z0, j1], T.z1[:], T.z0[:], T.tj192[:, 0:12], Op.mult)
-    b2 = scan([b1], T.B1[:], T.rm[:], T.A1[:], 0.0, Op.mult, Op.add)
-    z2 = tt([z0, j2], T.z2[:], T.z0[:], T.tjtr[:, 0:12], Op.mult)
+    a0 = tc([dtab, ft], T.T1[:, 0:12], T.tb[:])
+    a1 = ts([dtab], T.T1[:, 14:26], T.tb[:], 0.0, Op.is_gt)
+    b1 = do("v", [a1, fr], lambda: V.transpose(T.A1[:, 32:96], T.T1[:]))
+    drow = dma("s", "drow", T.row1[0:1, :], T.A1[0:12, 32:48], [b1])
+    dw0 = dma("s", "dw0", T.wt[:, 0:1536], T.w[:, 0:1536])
+    dw1 = dma("s", "dw1", T.wt[:, 1536:3072], T.w[:, 1536:3072])
+    z0 = ts([a1], T.z0[:], T.T1[:, 0:26], 0.0, Op.is_equal)
+    b2 = scan([b1], T.B1[:], T.A1[:, 31:95], T.rm[:], 0.0, Op.add, Op.mult)
+    zz = tt([z0, jj], T.zz[:], T.z0[:], T.tjj[:], Op.mult)
     b3 = do("v", [b2], lambda: V.transpose(T.Z1[:], T.B1[:]))
-    nn = scan([b3], T.cn[:, 1:13], T.Z1[:, 96:108], T.T1[:, 12:24], -1.0, Op.add, Op.add)
-    tot = scan([b3], T.cc[:, 1:13], T.Z1[:, 32:44], T.T1[:, 12:24], 0.0, Op.add, Op.add)
-    hi = list(range(r + 1, N))
-    if hi:
-        fused([tot], [(hi, E, "atot", T.cc[:, 12:13], [T.tl[:, 8 - d + r:9 - d + r] for d in hi])])
-    o = tt([nn], T.o1[:], T.Z1[:, 64:76], T.cn[:, 0:12], Op.add)
-    s1 = tt([tot], T.s1[:], T.Z1[:, 0:12], T.cc[:, 0:12], Op.add)
-    o = tt([o, z1], T.o2[:], T.o1[:], T.z1[:], Op.max)
-    s1 = tt([s1], T.s2[:], T.s1[:], T.T1[:, 0:12], Op.subtract)
-    o = tc([o], T.ok[:], T.o2[:])
-    qx = do("v", [dx], lambda: V.quantize_mx(T.raw[:, 0:C], T.raws[:, 0:C], T.xt[:, 0:4 * C]))
-    ks = tc([o, kr], T.kr[:, 0:2 * C].indirect(T.ok[:, 0:12]), T.ir[:, 0:C])
-    sx = tt([s1, z2], T.sx[:], T.s2[:], T.z2[:], Op.max)
-    f2 = ts([nn], T.f2[:], T.cn[:, 12:13], H - 1.0, Op.subtract, 0.0, Op.max)
-    kd = diag([ks, mk], T.kd[:], T.kr[:, 0:C], C)
-    sxu = tc([sx], T.sxu[:], T.sx[:])
+    ee = scan([b3, fz], T.ee[:, 1:27], T.rs[:], T.Z1[:, 32:58], 0.0, Op.mult, Op.add)
+    uu = tt([b3, zz], T.uu[:], T.Z1[:, 0:26], T.zz[:], Op.add)
+    to = [d for d in range(N) if d != r and slot(r, d) is not None]
+    if to:
+        fused([ee], [(to, E, "atot", T.ee[:, 12:13], [T.tl[:, slot(r, d):slot(r, d) + 1] for d in to])])
+    sx = tt([uu, ee], T.sx[:], T.uu[:], T.ee[:, 0:26], Op.add)
+    f2 = act([ee], T.f2[:], T.ee[:, 26:27], Act.Relu, bias=-float(H))
+    if r >= half:
+        fs = act([ee], T.tl[:, half + 1:half + 2], T.ee[:, 12:13])
+    i1 = act([k3], T.ir[:, C:2 * C], T.ir[:, 0:C], Act.Identity, bias=float(C))
+    act([i1], T.pw[:, W0 - 16:W0 + P - 16], T.ir[:, 0:P], scale=0.0)
+    fp = act([i1], T.pw[:, W0 + P - 16:W0 + P], T.ir[:, 0:16], scale=0.0)
+    sxu = tc([sx], T.su[:], T.sx[:])
+    ks = tc([sxu, kr], T.kr[:].indirect(T.su[:, 14:26]), T.ir[:, 0:C])
     if hi2 is not None:
         l2 = ts([f2, j0], T.l2[:, 0:7], T.tj[:, 0:7], T.f2[:], Op.add)
-    kl = ts([kd], T.kl[:], T.kd[:, 15:C:16], C - 1.0, Op.min)
-    ke = tc([kd], T.ke[:], T.kd[:, 15:C:16])
-    cq = pick([kl, qx], T.comp[:, 0:C], T.raw[:, 0:C], T.kl[:, 0:12])
-    cr = tc([pb, c12], T.cr[:], T.rowi[:, 0:C].indirect(T["ord"][:, 0:12]))
-    if hi2 is not None:
-        q2 = pick([l2, cq], T.sel2[:, 0:H], T.comp[:, 0:C], T.l2[:, 0:7])
-    er = scan([cr], T.er[:, 1:C], T.cr[:, 0:C - 1], T.cr[:, 0:C - 1], 0.0, Op.add, Op.max)
-    qw0 = do("v", [dw0], lambda: V.quantize_mx(T.wq[:, 0:384], T.ws[:, 0:384], T.wt[:, 0:1536]))
-    cs = act([kl, qx], T.comps[:, 0:C], T.raws[:, 0:C].indirect(T.kl[:, 0:12]))
-    sp = act([k3], T.sc[:, C:C + 128], T.ir[:, 0:128], Act.Identity, bias=tr + C)
-    sc = act([er, ep, ke], T.sc[:, 0:C], T.er[:, 0:2 * C].indirect(T.ke[:, 0:12]))
-    if hi2 is not None:
-        q2s = act([l2, cs], T.sel2s[:, 0:H], T.comps[:, 0:C].indirect(T.l2[:, 0:7]))
-        r2 = act([sc, l2], T.r2[:], T.sc[:, 0:C].indirect(T.l2[:, 0:7]))
+    kd = diag([ks, mk], T.kd[:], T.kr[:, 0:C], C)
+    qx = do("v", [dx], lambda: V.quantize_mx(T.raw[:, 0:C], T.raws[:, 0:C], T.xt[:, 0:4 * C]))
 
     ma, pa = me[r][0], seg(pt)[r][0]
+    fused([sxu], [([pt], E, "apt", T.su[:, 0:12], [T.pt[:]])])
+    pb = do("g", [drow], lambda: g.partition_broadcast(T.row[:], T.row1[0:1, :], 128))
     fused([qx], [([pt], E, "apc", codes(T.raw[:, 0:C]), [codes(T.win[:, pa:pa + C])])])
     fused([qx], [([pt], E, "apc", T.raws[:, 0:C], [T.wins[:, pa:pa + C]])])
     dma("s", "down", codes(T.win[:, ma:ma + C]), codes(T.raw[:, 0:C]), [qx])
     down = dma("s", "down", T.wins[:, ma:ma + C], T.raws[:, 0:C], [qx])
-    src = {}
-    if lo2 is not None:
-        src[lo2] = (T.comp, T.comps, cq, cs)
-    if hi2 is not None:
-        src[hi2] = (T.sel2, T.sel2s, q2, q2s)
-    at = {d: seg(d)[r][0] for d in seg(r)}
-    fused([src[d][2] for d in src], [([d], share(r, d), "acd", codes(src[d][0][:, 0:H]), [codes(T.win[:, at[d]:at[d] + H])]) for d in src])
-    fused([sxu], [([pt], E, "apt", T.sxu[:], [T.pt[:]])])
-    fused([src[d][3] for d in src], [([d], share(r, d), "acd", src[d][1][:, 0:H], [T.wins[:, at[d]:at[d] + H]]) for d in src])
 
-    tabs = {}
+    kl = ts([kd], T.kl[:], T.kd[:, 15:C:16], C - 1.0, Op.min)
+    ke = tc([kd], T.ke[:], T.kd[:, 15:C:16])
+    er = scan([pb], T.er[:, 1:C], T.row[:, 0:C - 1], T.row[:, 0:C - 1], 0.0, Op.add, Op.max)
+    cq = pick([kl, qx], T.comp[:, 0:C], T.raw[:, 0:C], T.kl[:, 0:12])
+    sc = act([er, e0, ep, ke], T.sc[:, 0:C], T.er[:, 0:2 * C].indirect(T.ke[:, 0:12]))
+    if hi2 is not None:
+        q2 = pick([l2, cq], T.sel2[:, 0:H], T.comp[:, 0:C], T.l2[:, 0:7])
+        r2 = act([sc, l2], T.r2[:], T.sc[:, 0:C].indirect(T.l2[:, 0:7]))
+
+    na = sum(len(eng(s)) for s in range(N) if s != r and slot(s, r) is not None)
+    a, b = half - len(summed(r)), half + 1 if r < half else half + 2
+    tS = act([fs] + ([("atot", na)] if na else []), T.js[:, 0:b - a], T.tl[:, a:b], scale=1.0 if r < half else -1.0, accum_out=T.S[:])
+    if z is not None:
+        ac = act([tS, sc], T.jk[:, 0:C - H], T.sc[:, 1:C - H + 1], Act.Sign, bias=T.S[:], accum_out=T.acc[:])
+    cs = act([kl, qx], T.comps[:, 0:C], T.raws[:, 0:C].indirect(T.kl[:, 0:12]))
+    src, scl, tabs = {}, {}, {}
     if lo2 is not None:
+        src[lo2] = (T.comp, cq)
         tabs[lo2] = (T.t0, T.d0, diag([sc], T.d0[:], T.sc[:, 0:H], H))
     if hi2 is not None:
+        src[hi2] = (T.sel2, q2)
         tabs[hi2] = (T.t2, T.d2, diag([r2], T.d2[:], T.r2[:], H))
-    if r > 0:
-        na = sum(len(eng(s)) for s in range(r))
-        tS = do("v", [("atot", na), fs], lambda: V.tensor_reduce(T.S[:], T.tl[:, 8 - r:9], AxisListType.X, Op.add))
-    if z is not None:
-        ac = act([tS, sc, sp], T.jk[:], T.sc[:, 1:C + 1], Act.Sign, bias=T.S[:], accum_out=T.acc[:])
+    at = {d: seg(d)[r][0] for d in seg(r)}
+    fused([src[d][1] for d in src], [([d], share(r, d), "acd", codes(src[d][0][:, 0:H]), [codes(T.win[:, at[d]:at[d] + H])]) for d in src])
 
     def base(d):
         return float(W0 - P * d) - shift
 
+    if z is not None:
+        le = ts([ac, j3], T.lze[:, 0:7], T.m2[:, 0:7], T.acc[:], Op.add, -0.5, Op.mult)
+        rz = act([le], T.rz[:], T.sc[:, 0:C].indirect(T.lze[:, 0:7]))
+    if lo2 is not None:
+        scl[lo2] = (T.comps, cs)
+    if hi2 is not None:
+        scl[hi2] = (T.sel2s, act([l2, cs], T.sel2s[:, 0:H], T.comps[:, 0:C].indirect(T.l2[:, 0:7])))
+    if z is not None:
+        qzs = act([le, cs], T.selzs[:, 0:H], T.comps[:, 0:C].indirect(T.lze[:, 0:7]))
     tk = {}
     for d in tabs:
         t, dd, tok = tabs[d]
         tk[d] = ts([tok, tS], t[:, 0:7], dd[:, 15:H:16], T.S[:], Op.add, base(d), Op.add)
     fused([tk[d] for d in tk], [([d], share(r, d), "act", tabs[d][0][:, 0:7], [T.ct[:, 7 * two(d).index(r):7 * two(d).index(r) + 7]]) for d in tk])
-    oa, ob = (0, 12) if pt > r else (12, 0)
-    oo = ts([tS, sx], T.po[:, oa:oa + 12], T.sx[:], T.S[:], Op.add, base(r), Op.add)
-    if pt > r:
-        pc = tt([tS], T.pc[:], T.S[:], T.cc[:, 12:13], Op.add)
-    else:
-        pc = tt([tS], T.pc[:], T.S[:], T.tl[:, 7:8], Op.subtract)
-    qw1 = do("v", [dw1], lambda: V.quantize_mx(T.wq[:, 384:768], T.ws[:, 384:768], T.wt[:, 1536:3072]))
     if z is not None:
-        le = ts([ac, j3], T.lze[:, 0:7], T.m2[:, 0:7], T.acc[:], Op.add, -0.5, Op.mult)
-        rz = act([le], T.rz[:], T.sc[:, 0:C + 128].indirect(T.lze[:, 0:7]))
-        lc = ts([le], T.lzc[:, 0:7], T.lze[:, 0:7], C - 1.0, Op.min)
-        qzs = act([lc, cs], T.selzs[:, 0:H], T.comps[:, 0:C].indirect(T.lzc[:, 0:7]))
-        qz = pick([lc, cq], T.selz[:, 0:H], T.comp[:, 0:C], T.lzc[:, 0:7])
+        qz = pick([le, cq], T.selz[:, 0:H], T.comp[:, 0:C], T.lze[:, 0:7])
         u = diag([rz], T.dz[:], T.rz[:], H)
+    oo = ts([tS, sx], T.po[:, 0:12], T.sx[:, 0:12], T.S[:], Op.add, base(r), Op.add)
+    if z is not None:
         tz = ts([u], T.tz[:, 0:7], T.dz[:, 15:H:16], T.S[:], Op.add, base(z), Op.add)
         fused([qz], [([z], E, "acd", codes(T.selz[:, 0:H]), [codes(T.win[:, at[z]:at[z] + H])])])
         fused([tz], [([z], E, "acz", T.tz[:, 0:7], [T.cz[:, 0:7]])])
+    fused([scl[d][1] for d in scl], [([d], share(r, d), "acd", scl[d][0][:, 0:H], [T.wins[:, at[d]:at[d] + H]]) for d in scl])
+    if z is not None:
         fused([qzs], [([z], E, "acd", T.selzs[:, 0:H], [T.wins[:, at[z]:at[z] + H]])])
 
-    act([i1], T.pw[:, W0 - 16:W0 + P - 16], T.ir[:, 0:P], scale=0.0)
-    fp = act([i1], T.pw[:, W0 + P - 16:W0 + P], T.ir[:, 0:16], scale=0.0)
+    if pt > r:
+        pc = act([tS, ee], T.pc[:], T.ee[:, 12:13], Act.Identity, bias=T.S[:])
+    else:
+        pc = act([tS], T.pc[:], T.tl[:, slot(pt, r):slot(pt, r) + 1], Act.Identity, scale=-1.0, bias=T.S[:])
     ir = act([i1], T.ir[:, 2 * C:WIN], T.ir[:, 0:WIN - 2 * C], Act.Identity, bias=2.0 * C)
     for k, s in enumerate(two(r)):
         vz = act([ir], T.vz[:, H * k:H * k + H], T.ir[:, me[s][0]:me[s][0] + H])
-    po = ts([pc, ("apt", len(eng(pt)))], T.po[:, ob:ob + 12], T.pt[:], T.pc[:], Op.add, base(r), Op.add)
-    a = min(me[r][0], me[pt][0])
-    pp = tc([oo, po, fp, ir], T.pw[:].indirect(T.po[:, 0:24]), T.ir[:, a:a + 2 * C])
+    pp = tc([oo, fp, i1 if me[r][0] + C <= 2 * C else ir], T.pw[:].indirect(T.po[:, 0:12]), T.ir[:, me[r][0]:me[r][0] + C])
+    po = ts([pc, ("apt", len(eng(pt)))], T.po[:, 12:24], T.pt[:], T.pc[:], Op.add, base(r), Op.add)
+    pp = tc([pp, po, ir], T.pw[:].indirect(T.po[:, 12:24]), T.ir[:, me[pt][0]:me[pt][0] + C])
+    qw0 = do("v", [dw0], lambda: V.quantize_mx(T.wq[:, 0:384], T.ws[:, 0:384], T.wt[:, 0:1536]))
     nt = len(two(r))
     pp = tc([pp, vz, ("act", sum(len(share(s, r)) for s in two(r)))], T.pw[:].indirect(T.ct[:, 0:7 * nt]), T.vz[:, 0:H * nt])
+    qw1 = do("v", [dw1], lambda: V.quantize_mx(T.wq[:, 384:768], T.ws[:, 384:768], T.wt[:, 1536:3072]))
     if z is not None:
         pp = tc([pp, ("acz", len(eng(z)))], T.pw[:].indirect(T.cz[:, 0:7]), T.ir[:, me[z][0]:me[z][0] + H])
-    h = 128 + 16
-    u = scan([pp], T.pm[:, 0:h], T.pw[:, W0 - 16:W0 + 128], T.pw[:, W0 - 16:W0 + 128], 0.0, Op.max, Op.max)
-    v = scan([u], T.pm[:, h:P + 16], T.pw[:, W0 + 128:W0 + P], T.pw[:, W0 + 128:W0 + P], T.pm[:, h - 1:h], Op.max, Op.max)
-    u = diag([u], T.pd[:, 0:128], T.pm[:, 16:h], 128)
-    v = diag([v], T.pd[:, 128:P], T.pm[:, h:P + 16], P - 128)
-    u = tc([u], T.il[:, 0:8], T.pd[:, 15:128:16])
-    v = tc([v], T.il[:, 8:24], T.pd[:, 143:P:16])
 
     ncd = sum(2 * len(share(s, r)) for s in two(r)) + (2 * len(eng(z)) if z is not None else 0)
     got = [down, ("apc", 2 * len(eng(pt))), ("acd", ncd)]
-    picks = []
-    for b in range(NB):
+
+    def run(b, dep):
+        lo = 0 if b == 0 else 16 + 128 * b
+        x = 16 + 128 * b + 128
+        pw = T.pw[:, W0 - 16 + lo:W0 - 16 + x]
+        return scan([dep], T.pm[:, lo:x], pw, pw, 0.0 if b == 0 else T.pm[:, lo - 1:lo], Op.max, Op.max)
+
+    def dg(b, dep):
+        return diag([dep], T.pd[:, 128 * b:128 * b + 128], T.pm[:, 16 + 128 * b:144 + 128 * b], 128)
+
+    def lst(b, dep):
+        return tc([dep], T.il[:, 8 * b:8 * b + 8], T.pd[:, 128 * b + 15:128 * b + 128:16])
+
+    def fin(b, dep):
         i = slice(128 * b, 128 * b + 128)
         o = T.il[:, 8 * b:8 * b + 8]
-        l = [v if b else u] + got
-        picks.append((pick(l, T.fin[:, i], T.win[:], o), act(l, T.fins[:, i], T.wins[:].indirect(o))))
-    for b in range(NB):
+        return [pick([dep] + got, T.fin[:, i], T.win[:], o), act([dep] + got, T.fins[:, i], T.wins[:].indirect(o))]
+
+    def mul(b, h, deps):
+        k = NO * b + h
+        wi = slice(128 * k, 128 * k + 128)
         i = slice(128 * b, 128 * b + 128)
-        for h in range(NO):
-            k = NO * b + h
-            wi = slice(128 * k, 128 * k + 128)
-            mm = do("t", list(picks[b]) + [qw0, qw1], lambda: g.tensor.matmul_mx(
-                T.ps[:, 512 * k:512 * k + 128], T.wq[:, wi], T.ws[:, wi], T.fin[:, i], T.fins[:, i], True, True))
-            yi = slice(P * h + 128 * b, P * h + 128 * b + 128)
-            cp = tc([mm], T.ysb[:, yi], T.ps[:, 512 * k:512 * k + 128]) if h == 0 else act([mm], T.ysb[:, yi], T.ps[:, 512 * k:512 * k + 128])
-            dma("s", "dy", T.y[:, yi], T.ysb[:, yi], [cp])
+        return do("t", deps + [qw0, qw1], lambda: g.tensor.matmul_mx(
+            T.ps[:, 512 * k:512 * k + 128], T.wq[:, wi], T.ws[:, wi], T.fin[:, i], T.fins[:, i], True, True))
+
+    def out(b, h, mm):
+        k = NO * b + h
+        yi = slice(P * h + 128 * b, P * h + 128 * b + 128)
+        cp = tc([mm], T.ysb[:, yi], T.ps[:, 512 * k:512 * k + 128]) if h == 0 else act([mm], T.ysb[:, yi], T.ps[:, 512 * k:512 * k + 128])
+        dma("s", "dy", T.y[:, yi], T.ysb[:, yi], [cp])
+
+    m0 = run(0, pp)
+    m1 = run(1, m0)
+    d0 = dg(0, m0)
+    m2 = run(2, m1)
+    l0 = lst(0, d0)
+    d1 = dg(1, m1)
+    c0 = fin(0, l0)
+    y0 = [mul(0, h, c0) for h in range(NO)]
+    l1 = lst(1, d1)
+    d2 = dg(2, m2)
+    c1 = fin(1, l1)
+    y1 = [mul(1, h, c1) for h in range(NO)]
+    l2 = lst(2, d2)
+    for h in range(NO):
+        out(0, h, y0[h])
+    c2 = fin(2, l2)
+    y2 = [mul(2, h, c2) for h in range(NO)]
+    for h in range(NO):
+        out(1, h, y1[h])
+    for h in range(NO):
+        out(2, h, y2[h])
 
     need("s", [("dy", total["dy"])])
     g.wait_ge(T.sem.sent, sent[0])

@@ -20,17 +20,17 @@ SCRATCH = {
     "sel2": sb(H, F8), "sel2s": sb(H, U8), "selz": sb(H, F8), "selzs": sb(H, U8),
     "win": sb(WIN, F8), "wins": sb(WIN, U8), "fin": sb(P, F8), "fins": sb(P, U8),
     "pi": sb(1, I32), "pa": sb(1, I32), "pf": sb(1, F32), "c16": sb(16, F32), "tj": sb(16, F32), "tji": sb(26, I32),
-    "tjj": sb(26, I32), "m2": sb(16, F32), "ir": sb(WIN, F32), "vz": sb(2 * H, F32), "mi": sb(16, I32), "mj": sb(16, I32),
-    "mask": sb(P, F32), "rm": sb(64, BF), "rs": sb(26, F32),
+    "tjj": sb(26, I32), "m2": sb(16, F32), "ir": sb(C, F32), "op": sb(2 * C, F32), "vz": sb(2 * H, F32), "zi": sb(H, F32),
+    "mi": sb(16, I32), "mj": sb(16, I32), "mask": sb(P, F32), "rm": sb(64, BF), "rs": sb(26, F32),
     "tb": sb(12, I32), "row1": sb(C, BF), "row": sb(C, BF), "T1": sb(64, BF), "A1": sb(96, BF), "B1": sb(64, BF),
     "Z1": sb(64, BF), "ee": sb(27, F32), "uu": sb(26, F32), "z0": sb(26, F32), "zz": sb(26, F32),
-    "sx": sb(26, F32), "su": sb(26, U16), "kr": sb(7680, F32), "kd": sb(C, F32), "kl": sb(12, U16), "ke": sb(12, U16),
+    "sx": sb(26, F32), "su": sb(26, U16), "kr": sb(11776, F32), "kd": sb(C, F32), "kl": sb(12, U16), "ke": sb(12, U16),
     "er": sb(2 * C, F32), "sc": sb(C, F32),
     "f2": sb(1, F32), "l2": sb(8, U16), "r2": sb(H, F32), "d0": sb(H, F32), "d2": sb(H, F32), "dz": sb(H, F32),
     "t0": sb(8, U16), "t2": sb(8, U16), "tz": sb(8, U16), "rz": sb(H, F32),
     "tl": sb(12, F32), "S": sb(1, F32), "pc": sb(1, F32), "jk": sb(C, F32), "js": sb(8, F32), "acc": sb(1, F32),
     "lze": sb(8, U16), "pt": sb(12, U16), "po": sb(24, U16), "ct": sb(16, U16), "cz": sb(8, U16),
-    "pw": sb(11264, F32), "pm": sb(P + 16, F32), "pd": sb(P, F32), "il": sb(24, U16),
+    "pw": sb(14336, F32), "pm": sb(P + 16, F32), "pd": sb(P, F32), "il": sb(24, U16),
     "ysb": sb(NO * P, F32), "ps": ("psum", [128, 512 * 6], F32),
 }
 SEMAPHORES = ["sv", "sa", "sg", "st", "dtab", "drow", "dx", "dw0", "dw1", "down", "dy", "sent",
@@ -78,6 +78,9 @@ def rank_program(g, core, T, topo):
 
     def eng(q):
         return common(topo, cores[q], [c for c in cores if c != cores[q]])
+
+    def inner(q):
+        return [e for e in topo.engines(cores[q], cores[partner(q)]) if e not in eng(q)] or eng(q)
 
     def share(q, d):
         e, v = eng(q), two(q)
@@ -157,8 +160,16 @@ def rank_program(g, core, T, topo):
     def pick(deps, out, in_, o):
         return tc(deps, out.bitcast(dt.uint32), in_.bitcast(dt.uint32).indirect(o))
 
+    def quant(i, j, d):
+        return do("v", [d], lambda: V.quantize_mx(T.wq[:, i:j], T.ws[:, i:j], T.wt[:, 4 * i:4 * j]))
+
     def codes(ap):
         return ap.bitcast(dt.uint8)
+
+    shift = -P * z - 0.5 if z is not None else 0.0
+
+    def base(d):
+        return float(W0 - P * d) - shift
 
     for k in range(8):
         dtab = dma("s" if k % 2 == 0 else "a", "dtab", T.tb[16 * k:16 * k + 16, :], T.cnt[:])
@@ -168,7 +179,7 @@ def rank_program(g, core, T, topo):
     k4 = do("g", (), lambda: g.iota(T.mi[:], [[1, 16]], 0, 15))
     k1 = do("g", (), lambda: g.iota(T.c16[:], [[16, 16]], 0, 0, **flag))
     k0 = do("g", (), lambda: g.iota(T.pi[:], [[0, 1]], 0, 1))
-    k5 = do("g", (), lambda: g.iota(T.tji[:], [[128, 26]], FAR, 1))
+    k5 = do("g", (), lambda: g.iota(T.tji[:], [[128, 26]], FAR * (1 + r % 2), 1))
     k3 = do("g", (), lambda: g.iota(T.ir[:, 0:C], [[1, C]], 0, 0, **flag))
     ft = fill(T.T1[:], 0.0)
     u = fill(T.rm[:], 1.0)
@@ -183,7 +194,6 @@ def rank_program(g, core, T, topo):
     def const(deps, out, c):
         return act([k1] + list(deps), out, T.c16[:, 0:1], Act.Identity, scale=0.0, bias=float(c))
 
-    shift = -P * z - 0.5 if z is not None else 0.0
     fs = const((), T.tl[:, half:half + 1], shift if r < half else -(N * P + shift))
     e0 = const((), T.er[:, 0:1], 0)
     fz = const((), T.ee[:, 0:1], 0)
@@ -222,9 +232,14 @@ def rank_program(g, core, T, topo):
     f2 = act([ee], T.f2[:], T.ee[:, 26:27], Act.Relu, bias=-float(H))
     if r >= half:
         fs = act([ee], T.tl[:, half + 1:half + 2], T.ee[:, 12:13])
-    i1 = act([k3], T.ir[:, C:2 * C], T.ir[:, 0:C], Act.Identity, bias=float(C))
-    act([i1], T.pw[:, W0 - 16:W0 + P - 16], T.ir[:, 0:P], scale=0.0)
-    fp = act([i1], T.pw[:, W0 + P - 16:W0 + P], T.ir[:, 0:16], scale=0.0)
+    act([mk], T.pw[:, W0 - 16:W0 + P - 16], T.mask[:, 0:P], scale=0.0)
+    fp = act([mk], T.pw[:, W0 + P - 16:W0 + P], T.mask[:, 0:16], scale=0.0)
+    for k, s in enumerate((r, pt)):
+        op = act([k3], T.op[:, C * k:C * k + C], T.ir[:], Act.Identity, bias=float(me[s][0]))
+    for k, s in enumerate(two(r)):
+        vz = act([k3], T.vz[:, H * k:H * k + H], T.ir[:, 0:H], Act.Identity, bias=float(me[s][0]))
+    if z is not None:
+        zi = act([k3], T.zi[:], T.ir[:, 0:H], Act.Identity, bias=float(me[z][0]))
     sxu = tc([sx], T.su[:], T.sx[:])
     ks = tc([sxu, kr], T.kr[:].indirect(T.su[:, 14:26]), T.ir[:, 0:C])
     if hi2 is not None:
@@ -233,10 +248,8 @@ def rank_program(g, core, T, topo):
     qx = do("v", [dx], lambda: V.quantize_mx(T.raw[:, 0:C], T.raws[:, 0:C], T.xt[:, 0:4 * C]))
 
     ma, pa = me[r][0], seg(pt)[r][0]
-    fused([sxu], [([pt], E, "apt", T.su[:, 0:12], [T.pt[:]])])
     pb = do("g", [drow], lambda: g.partition_broadcast(T.row[:], T.row1[0:1, :], 128))
-    fused([qx], [([pt], E, "apc", codes(T.raw[:, 0:C]), [codes(T.win[:, pa:pa + C])])])
-    fused([qx], [([pt], E, "apc", T.raws[:, 0:C], [T.wins[:, pa:pa + C]])])
+    fused([sxu], [([pt], E, "apt", T.su[:, 0:12], [T.pt[:]])])
     dma("s", "down", codes(T.win[:, ma:ma + C]), codes(T.raw[:, 0:C]), [qx])
     down = dma("s", "down", T.wins[:, ma:ma + C], T.raws[:, 0:C], [qx])
 
@@ -244,29 +257,34 @@ def rank_program(g, core, T, topo):
     ke = tc([kd], T.ke[:], T.kd[:, 15:C:16])
     er = scan([pb], T.er[:, 1:C], T.row[:, 0:C - 1], T.row[:, 0:C - 1], 0.0, Op.add, Op.max)
     cq = pick([kl, qx], T.comp[:, 0:C], T.raw[:, 0:C], T.kl[:, 0:12])
+    cs = act([kl, qx], T.comps[:, 0:C], T.raws[:, 0:C].indirect(T.kl[:, 0:12]))
     sc = act([er, e0, ep, ke], T.sc[:, 0:C], T.er[:, 0:2 * C].indirect(T.ke[:, 0:12]))
+    src, scl, tabs, tk = {}, {}, {}, {}
     if hi2 is not None:
         q2 = pick([l2, cq], T.sel2[:, 0:H], T.comp[:, 0:C], T.l2[:, 0:7])
+        src[hi2] = (T.sel2, q2)
         r2 = act([sc, l2], T.r2[:], T.sc[:, 0:C].indirect(T.l2[:, 0:7]))
+    if lo2 is not None:
+        src[lo2] = (T.comp, cq)
+    at = {d: seg(d)[r][0] for d in seg(r)}
+    fused([src[d][1] for d in two(r)], [([d], share(r, d), "acd", codes(src[d][0][:, 0:H]), [codes(T.win[:, at[d]:at[d] + H])]) for d in two(r)])
+    fused([qx], [([pt], inner(r), "apc", codes(T.raw[:, 0:C]), [codes(T.win[:, pa:pa + C])])])
+    fused([qx], [([pt], inner(r), "apc", T.raws[:, 0:C], [T.wins[:, pa:pa + C]])])
 
     na = sum(len(eng(s)) for s in range(N) if s != r and slot(s, r) is not None)
     a, b = half - len(summed(r)), half + 1 if r < half else half + 2
     tS = act([fs] + ([("atot", na)] if na else []), T.js[:, 0:b - a], T.tl[:, a:b], scale=1.0 if r < half else -1.0, accum_out=T.S[:])
     if z is not None:
         ac = act([tS, sc], T.jk[:, 0:C - H], T.sc[:, 1:C - H + 1], Act.Sign, bias=T.S[:], accum_out=T.acc[:])
-    cs = act([kl, qx], T.comps[:, 0:C], T.raws[:, 0:C].indirect(T.kl[:, 0:12]))
-    src, scl, tabs = {}, {}, {}
+    if pt > r:
+        pc = act([tS, ee], T.pc[:], T.ee[:, 12:13], Act.Identity, bias=T.S[:])
+    else:
+        pc = act([tS], T.pc[:], T.tl[:, slot(pt, r):slot(pt, r) + 1], Act.Identity, scale=-1.0, bias=T.S[:])
     if lo2 is not None:
-        src[lo2] = (T.comp, cq)
         tabs[lo2] = (T.t0, T.d0, diag([sc], T.d0[:], T.sc[:, 0:H], H))
     if hi2 is not None:
-        src[hi2] = (T.sel2, q2)
         tabs[hi2] = (T.t2, T.d2, diag([r2], T.d2[:], T.r2[:], H))
-    at = {d: seg(d)[r][0] for d in seg(r)}
-    fused([src[d][1] for d in src], [([d], share(r, d), "acd", codes(src[d][0][:, 0:H]), [codes(T.win[:, at[d]:at[d] + H])]) for d in src])
-
-    def base(d):
-        return float(W0 - P * d) - shift
+    qw = [quant(0, 384, dw0), quant(384, 768, dw1)]
 
     if z is not None:
         le = ts([ac, j3], T.lze[:, 0:7], T.m2[:, 0:7], T.acc[:], Op.add, -0.5, Op.mult)
@@ -277,65 +295,50 @@ def rank_program(g, core, T, topo):
         scl[hi2] = (T.sel2s, act([l2, cs], T.sel2s[:, 0:H], T.comps[:, 0:C].indirect(T.l2[:, 0:7])))
     if z is not None:
         qzs = act([le, cs], T.selzs[:, 0:H], T.comps[:, 0:C].indirect(T.lze[:, 0:7]))
-    tk = {}
     for d in tabs:
         t, dd, tok = tabs[d]
         tk[d] = ts([tok, tS], t[:, 0:7], dd[:, 15:H:16], T.S[:], Op.add, base(d), Op.add)
-    fused([tk[d] for d in tk], [([d], share(r, d), "act", tabs[d][0][:, 0:7], [T.ct[:, 7 * two(d).index(r):7 * two(d).index(r) + 7]]) for d in tk])
+    fused([tk[d] for d in two(r)], [([d], share(r, d), "act", tabs[d][0][:, 0:7], [T.ct[:, 7 * two(d).index(r):7 * two(d).index(r) + 7]]) for d in two(r)])
     if z is not None:
         qz = pick([le, cq], T.selz[:, 0:H], T.comp[:, 0:C], T.lze[:, 0:7])
         u = diag([rz], T.dz[:], T.rz[:], H)
     oo = ts([tS, sx], T.po[:, 0:12], T.sx[:, 0:12], T.S[:], Op.add, base(r), Op.add)
     if z is not None:
         tz = ts([u], T.tz[:, 0:7], T.dz[:, 15:H:16], T.S[:], Op.add, base(z), Op.add)
-        fused([qz], [([z], E, "acd", codes(T.selz[:, 0:H]), [codes(T.win[:, at[z]:at[z] + H])])])
         fused([tz], [([z], E, "acz", T.tz[:, 0:7], [T.cz[:, 0:7]])])
-    fused([scl[d][1] for d in scl], [([d], share(r, d), "acd", scl[d][0][:, 0:H], [T.wins[:, at[d]:at[d] + H]]) for d in scl])
+        fused([qz], [([z], E, "acd", codes(T.selz[:, 0:H]), [codes(T.win[:, at[z]:at[z] + H])])])
+    fused([scl[d][1] for d in two(r)], [([d], share(r, d), "acd", scl[d][0][:, 0:H], [T.wins[:, at[d]:at[d] + H]]) for d in two(r)])
     if z is not None:
         fused([qzs], [([z], E, "acd", T.selzs[:, 0:H], [T.wins[:, at[z]:at[z] + H]])])
 
-    if pt > r:
-        pc = act([tS, ee], T.pc[:], T.ee[:, 12:13], Act.Identity, bias=T.S[:])
-    else:
-        pc = act([tS], T.pc[:], T.tl[:, slot(pt, r):slot(pt, r) + 1], Act.Identity, scale=-1.0, bias=T.S[:])
-    ir = act([i1], T.ir[:, 2 * C:WIN], T.ir[:, 0:WIN - 2 * C], Act.Identity, bias=2.0 * C)
-    for k, s in enumerate(two(r)):
-        vz = act([ir], T.vz[:, H * k:H * k + H], T.ir[:, me[s][0]:me[s][0] + H])
-    pp = tc([oo, fp, i1 if me[r][0] + C <= 2 * C else ir], T.pw[:].indirect(T.po[:, 0:12]), T.ir[:, me[r][0]:me[r][0] + C])
     po = ts([pc, ("apt", len(eng(pt)))], T.po[:, 12:24], T.pt[:], T.pc[:], Op.add, base(r), Op.add)
-    pp = tc([pp, po, ir], T.pw[:].indirect(T.po[:, 12:24]), T.ir[:, me[pt][0]:me[pt][0] + C])
-    qw0 = do("v", [dw0], lambda: V.quantize_mx(T.wq[:, 0:384], T.ws[:, 0:384], T.wt[:, 0:1536]))
+    pp = tc([oo, po, fp, op], T.pw[:].indirect(T.po[:, 0:24]), T.op[:])
     nt = len(two(r))
     pp = tc([pp, vz, ("act", sum(len(share(s, r)) for s in two(r)))], T.pw[:].indirect(T.ct[:, 0:7 * nt]), T.vz[:, 0:H * nt])
-    qw1 = do("v", [dw1], lambda: V.quantize_mx(T.wq[:, 384:768], T.ws[:, 384:768], T.wt[:, 1536:3072]))
     if z is not None:
-        pp = tc([pp, ("acz", len(eng(z)))], T.pw[:].indirect(T.cz[:, 0:7]), T.ir[:, me[z][0]:me[z][0] + H])
+        pp = tc([pp, zi, ("acz", len(eng(z)))], T.pw[:].indirect(T.cz[:, 0:7]), T.zi[:])
 
     ncd = sum(2 * len(share(s, r)) for s in two(r)) + (2 * len(eng(z)) if z is not None else 0)
-    got = [down, ("apc", 2 * len(eng(pt))), ("acd", ncd)]
+    got = [down, ("apc", 2 * len(inner(pt))), ("acd", ncd)]
 
-    def run(b, dep):
-        lo = 0 if b == 0 else 16 + 128 * b
-        x = 16 + 128 * b + 128
-        pw = T.pw[:, W0 - 16 + lo:W0 - 16 + x]
-        return scan([dep], T.pm[:, lo:x], pw, pw, 0.0 if b == 0 else T.pm[:, lo - 1:lo], Op.max, Op.max)
+    X = slice(W0 - 16, W0 + P)
+    m = scan([pp], T.pm[:], T.pw[:, X], T.pw[:, X], 0.0, Op.max, Op.max)
+    d0 = diag([m], T.pd[:, 0:128], T.pm[:, 16:144], 128)
+    d1 = diag([m], T.pd[:, 128:P], T.pm[:, 144:16 + P], P - 128)
+    l0 = tc([d0], T.il[:, 0:8], T.pd[:, 15:128:16])
+    l1 = tc([d1], T.il[:, 8:24], T.pd[:, 143:P:16])
 
-    def dg(b, dep):
-        return diag([dep], T.pd[:, 128 * b:128 * b + 128], T.pm[:, 16 + 128 * b:144 + 128 * b], 128)
-
-    def lst(b, dep):
-        return tc([dep], T.il[:, 8 * b:8 * b + 8], T.pd[:, 128 * b + 15:128 * b + 128:16])
-
-    def fin(b, dep):
+    def fin(b):
         i = slice(128 * b, 128 * b + 128)
         o = T.il[:, 8 * b:8 * b + 8]
-        return [pick([dep] + got, T.fin[:, i], T.win[:], o), act([dep] + got, T.fins[:, i], T.wins[:].indirect(o))]
+        dep = [l1 if b else l0] + got
+        return [pick(dep, T.fin[:, i], T.win[:], o), act(dep, T.fins[:, i], T.wins[:].indirect(o))]
 
     def mul(b, h, deps):
         k = NO * b + h
         wi = slice(128 * k, 128 * k + 128)
         i = slice(128 * b, 128 * b + 128)
-        return do("t", deps + [qw0, qw1], lambda: g.tensor.matmul_mx(
+        return do("t", deps + qw, lambda: g.tensor.matmul_mx(
             T.ps[:, 512 * k:512 * k + 128], T.wq[:, wi], T.ws[:, wi], T.fin[:, i], T.fins[:, i], True, True))
 
     def out(b, h, mm):
@@ -344,27 +347,13 @@ def rank_program(g, core, T, topo):
         cp = tc([mm], T.ysb[:, yi], T.ps[:, 512 * k:512 * k + 128]) if h == 0 else act([mm], T.ysb[:, yi], T.ps[:, 512 * k:512 * k + 128])
         dma("s", "dy", T.y[:, yi], T.ysb[:, yi], [cp])
 
-    m0 = run(0, pp)
-    m1 = run(1, m0)
-    d0 = dg(0, m0)
-    m2 = run(2, m1)
-    l0 = lst(0, d0)
-    d1 = dg(1, m1)
-    c0 = fin(0, l0)
-    y0 = [mul(0, h, c0) for h in range(NO)]
-    l1 = lst(1, d1)
-    d2 = dg(2, m2)
-    c1 = fin(1, l1)
-    y1 = [mul(1, h, c1) for h in range(NO)]
-    l2 = lst(2, d2)
-    for h in range(NO):
-        out(0, h, y0[h])
-    c2 = fin(2, l2)
-    y2 = [mul(2, h, c2) for h in range(NO)]
-    for h in range(NO):
-        out(1, h, y1[h])
-    for h in range(NO):
-        out(2, h, y2[h])
+    y = []
+    for b in range(NB):
+        c = fin(b)
+        y.append([mul(b, h, c) for h in range(NO)])
+    for b in range(NB):
+        for h in range(NO):
+            out(b, h, y[b][h])
 
     need("s", [("dy", total["dy"])])
     g.wait_ge(T.sem.sent, sent[0])

from concourse.bass import DstId, RemoteDMATransfer
from concourse.mybir import dt, AluOpType as Op, AxisListType, ActivationFunctionType as Act

C, P, NB, NO, H = 192, 384, 3, 2, 112
W0 = 1536
TR = 3584
FAR = 4096
BIG = 1.0e6
WIN = 3 * H + 2 * C
F32, I32, U16, U8, F8, BF = "float32", "int32", "uint16", "uint8", "float8_e4m3fn_x4", "bfloat16"


def sb(n, t):
    return ("sbuf", [128, n], t)


SCRATCH = {
    "xt": sb(4 * C, BF), "wt": sb(512 * 6, BF), "wq": sb(768, F8), "ws": sb(768, U8),
    "raw": sb(C, F8), "raws": sb(C, U8), "comp": sb(C, F8), "comps": sb(C, U8),
    "sel2": sb(H, F8), "sel2s": sb(H, U8), "selz": sb(H, F8), "selzs": sb(H, U8),
    "win": sb(WIN, F8), "wins": sb(WIN, U8), "fin": sb(P, F8), "fins": sb(P, U8),
    "pi": sb(1, I32), "pa": sb(1, I32), "pf": sb(1, F32), "c16": sb(16, F32), "tj": sb(16, F32), "tji": sb(26, I32),
    "tjj": sb(26, I32), "m2": sb(16, F32), "ir": sb(C, F32), "op": sb(2 * C, F32), "vz": sb(2 * H, F32), "zi": sb(H, F32),
    "mi": sb(16, I32), "mj": sb(16, I32), "mask": sb(P, F32), "rm": sb(64, BF), "rs": sb(26, F32),
    "tb": sb(12, I32), "row1": sb(C, BF), "row": sb(C, BF), "T1": sb(64, BF), "A1": sb(96, BF), "B1": sb(64, BF),
    "Z1": sb(64, BF), "ee": sb(27, F32), "uu": sb(26, F32), "z0": sb(26, F32), "zz": sb(26, F32),
    "sx": sb(26, F32), "su": sb(26, U16), "kr": sb(11776, F32), "kd": sb(C, F32), "kl": sb(12, U16), "ke": sb(12, U16),
    "er": sb(2 * C, F32), "sc": sb(C, F32),
    "f2": sb(1, F32), "l2": sb(8, U16), "r2": sb(H, F32), "d0": sb(H, F32), "d2": sb(H, F32), "dz": sb(H, F32),
    "t0": sb(8, U16), "t2": sb(8, U16), "tz": sb(8, U16), "rz": sb(H, F32),
    "tl": sb(12, F32), "S": sb(1, F32), "pc": sb(1, F32), "jk": sb(C, F32), "js": sb(8, F32), "acc": sb(1, F32),
    "lze": sb(8, U16), "pt": sb(12, U16), "po": sb(24, U16), "ct": sb(16, U16), "cz": sb(8, U16),
    "pw": sb(14336, F32), "pm": sb(P + 16, F32), "pd": sb(P, F32), "il": sb(24, U16),
    "ysb": sb(NO * P, F32), "ps": ("psum", [128, 512 * 6], F32),
}
SEMAPHORES = ["sv", "sa", "sg", "st", "dtab", "drow", "dx", "dw0", "dw1", "down", "dy", "sent",
              "atot", "apt", "apc", "act", "acz", "acd"]


def common(topo, src, dsts):
    e = topo.engines(src, dsts[0])
    for d in dsts[1:]:
        e = [k for k in e if k in topo.engines(src, d)]
    return e


def bits(e):
    m = 0
    for k in e:
        m |= 1 << k
    return m


def rank_program(g, core, T, topo):
    r = T.rank_of(core)
    if r is None:
        return
    cores = T.cores
    N = len(cores)
    half = N // 2

    def partner(q):
        return [d for d in (q - 1, q + 1) if 0 <= d < N and topo.chip(cores[d]) == topo.chip(cores[q])][0]

    def two(q):
        return [d for d in (q - 2, q + 2) if 0 <= d < N]

    def zed(q):
        return [d for d in (q - 1, q + 1) if 0 <= d < N and d != partner(q)]

    def seg(d):
        a, o = {}, 0
        for s in range(max(0, d - 2), min(N, d + 3)):
            n = C if s in (d, partner(d)) else H
            a[s] = (o, n)
            o += n
        return a

    def eng(q):
        return common(topo, cores[q], [c for c in cores if c != cores[q]])

    def inner(q):
        return [e for e in topo.engines(cores[q], cores[partner(q)]) if e not in eng(q)] or eng(q)

    def share(q, d):
        e, v = eng(q), two(q)
        n = len(e) // len(v)
        return e[n * v.index(d):n * v.index(d) + n]

    def summed(d):
        return list(range(d)) if d < half else list(range(d + 1, N))

    def slot(s, d):
        if s in summed(d):
            return half - len(summed(d)) + summed(d).index(s)
        return 2 * half if s == partner(d) and s < d else None

    pt, me, E = partner(r), seg(r), eng(r)
    lo2 = r - 2 if r - 2 >= 0 else None
    hi2 = r + 2 if r + 2 < N else None
    z = (zed(r) + [None])[0]
    tr = float(TR * (1 + (r + r // half) % 2))
    qs = {"v": g.vector, "a": g.scalar, "s": g.sync, "t": g.tensor, "g": g}
    home = {"v": "sv", "a": "sa", "t": "st", "g": "sg"}
    seen, total = {}, {}

    def need(q, toks):
        for sem, val in toks:
            if seen.get((q, sem), 0) < val:
                qs[q].wait_ge(T.sem[sem], val)
                seen[(q, sem)] = val

    def do(q, deps, fn, sem=None, n=1):
        need(q, deps)
        s = sem or home[q]
        fn().then_inc(T.sem[s], n)
        total[s] = total.get(s, 0) + n
        return (s, total[s])

    V, A = g.vector, g.scalar

    def dma(q, sem, out, in_, deps=()):
        return do(q, deps, lambda: qs[q].dma_start(out, in_), sem, 16)

    def dst(c):
        rid, pid, _ = topo.addr(c)
        return DstId(rid=rid, pnc=pid)

    sent = [0]

    def fused(deps, trs):
        need("g", deps)
        g.remote_dma_fused([RemoteDMATransfer(dst_ids=[dst(cores[d]) for d in ds], dma_engine_mask=bits(e), remote_sem=T.sem[sem],
                                              srcs=[a], dsts=b) for ds, e, sem, a, b in trs], local_sem=T.sem.sent)
        sent[0] += sum(len(e) for ds, e, sem, a, b in trs)

    def tc(deps, out, in_):
        return do("v", deps, lambda: V.tensor_copy(out, in_))

    def tt(deps, out, a, b, op):
        return do("v", deps, lambda: V.tensor_tensor(out, a, b, op))

    def ts(deps, out, a, s1, op0, s2=None, op1=None):
        if op1 is None:
            return do("v", deps, lambda: V.tensor_scalar(out, a, s1, None, op0))
        return do("v", deps, lambda: V.tensor_scalar(out, a, s1, s2, op0, op1))

    def scan(deps, out, a, b, init, op0, op1):
        return do("v", deps, lambda: V.tensor_tensor_scan(out, a, b, init, op0, op1))

    def diag(deps, out, row, n):
        return scan(deps, out, T.mask[:, 0:n], row, 0.0, Op.max, Op.min)

    def fill(ap, c):
        return do("v", (), lambda: V.memset(ap, c))

    def act(deps, out, in_, func=Act.Copy, **kw):
        return do("a", deps, lambda: A.activation(out, in_, func, **kw))

    def pick(deps, out, in_, o):
        return tc(deps, out.bitcast(dt.uint32), in_.bitcast(dt.uint32).indirect(o))

    def quant(i, j, d):
        return do("v", [d], lambda: V.quantize_mx(T.wq[:, i:j], T.ws[:, i:j], T.wt[:, 4 * i:4 * j]))

    def codes(ap):
        return ap.bitcast(dt.uint8)

    shift = -P * z - 0.5 if z is not None else 0.0

    def base(d):
        return float(W0 - P * d) - shift

    for k in range(8):
        dtab = dma("s" if k % 2 == 0 else "a", "dtab", T.tb[16 * k:16 * k + 16, :], T.cnt[:])
    dx = dma("a", "dx", T.xt[:], T.x[:])

    flag = {"allow_small_or_imprecise_dtypes": True}
    k4 = do("g", (), lambda: g.iota(T.mi[:], [[1, 16]], 0, 15))
    k1 = do("g", (), lambda: g.iota(T.c16[:], [[16, 16]], 0, 0, **flag))
    k0 = do("g", (), lambda: g.iota(T.pi[:], [[0, 1]], 0, 1))
    k5 = do("g", (), lambda: g.iota(T.tji[:], [[128, 26]], FAR * (1 + r % 2), 1))
    k3 = do("g", (), lambda: g.iota(T.ir[:, 0:C], [[1, C]], 0, 0, **flag))
    ft = fill(T.T1[:], 0.0)
    u = fill(T.rm[:], 1.0)
    v = ts([k4], T.mj[:], T.mi[:], 15, Op.bitwise_and)
    fill(T.A1[:, 31:32], 0.0)
    mk = ts([v], T.mask[:, 0:16], T.mj[:], 0.0, Op.is_equal, BIG, Op.mult)
    fr = do("v", [u], lambda: V.memset(T.rm[:, 0:32:16], 0.0))
    u = ts([k0], T.pa[:], T.pi[:], 15, Op.bitwise_and)
    jj = ts([k5], T.tjj[:], T.tji[:], 16383 - 127 + 15, Op.bitwise_and)
    pf = tc([u], T.pf[:], T.pa[:])

    def const(deps, out, c):
        return act([k1] + list(deps), out, T.c16[:, 0:1], Act.Identity, scale=0.0, bias=float(c))

    fs = const((), T.tl[:, half:half + 1], shift if r < half else -(N * P + shift))
    e0 = const((), T.er[:, 0:1], 0)
    fz = const((), T.ee[:, 0:1], 0)
    act([k1], T.rs[:, 0:13], T.c16[:, 0:13], Act.Identity, scale=0.0, bias=1.0)
    act([k1], T.rs[:, 14:26], T.c16[:, 0:12], Act.Identity, scale=0.0, bias=1.0)
    fz = const((), T.rs[:, 13:14], 0)
    n = 16
    while n < P:
        w = min(n, P - n)
        mk = act([mk], T.mask[:, n:n + w], T.mask[:, 0:w])
        n += w
        if n == 32:
            j0 = act([pf], T.tj[:], T.c16[:], Act.Identity, bias=T.pf[:])
        if n == 64:
            kr = act([k3], T.kr[:, 0:C], T.ir[:, 0:C], Act.Identity, bias=float(C))
            j3 = act([j0], T.m2[:], T.tj[:], Act.Identity, scale=-2.0, bias=-float(C - H))
        if n == 256:
            ep = act([k3], T.er[:, C:2 * C], T.ir[:, 0:C], Act.Identity, bias=tr)

    a0 = tc([dtab, ft], T.T1[:, 0:12], T.tb[:])
    a1 = ts([dtab], T.T1[:, 14:26], T.tb[:], 0.0, Op.is_gt)
    b1 = do("v", [a1, fr], lambda: V.transpose(T.A1[:, 32:96], T.T1[:]))
    drow = dma("s", "drow", T.row1[0:1, :], T.A1[0:12, 32:48], [b1])
    dw0 = dma("s", "dw0", T.wt[:, 0:1536], T.w[:, 0:1536])
    dw1 = dma("s", "dw1", T.wt[:, 1536:3072], T.w[:, 1536:3072])
    z0 = ts([a1], T.z0[:], T.T1[:, 0:26], 0.0, Op.is_equal)
    b2 = scan([b1], T.B1[:], T.A1[:, 31:95], T.rm[:], 0.0, Op.add, Op.mult)
    zz = tt([z0, jj], T.zz[:], T.z0[:], T.tjj[:], Op.mult)
    b3 = do("v", [b2], lambda: V.transpose(T.Z1[:], T.B1[:]))
    ee = scan([b3, fz], T.ee[:, 1:27], T.rs[:], T.Z1[:, 32:58], 0.0, Op.mult, Op.add)
    uu = tt([b3, zz], T.uu[:], T.Z1[:, 0:26], T.zz[:], Op.add)
    to = [d for d in range(N) if d != r and slot(r, d) is not None]
    if to:
        fused([ee], [(to, E, "atot", T.ee[:, 12:13], [T.tl[:, slot(r, d):slot(r, d) + 1] for d in to])])
    sx = tt([uu, ee], T.sx[:], T.uu[:], T.ee[:, 0:26], Op.add)
    f2 = act([ee], T.f2[:], T.ee[:, 26:27], Act.Relu, bias=-float(H))
    if r >= half:
        fs = act([ee], T.tl[:, half + 1:half + 2], T.ee[:, 12:13])
    act([mk], T.pw[:, W0 - 16:W0 + P - 16], T.mask[:, 0:P], scale=0.0)
    fp = act([mk], T.pw[:, W0 + P - 16:W0 + P], T.mask[:, 0:16], scale=0.0)
    for k, s in enumerate((r, pt)):
        op = act([k3], T.op[:, C * k:C * k + C], T.ir[:], Act.Identity, bias=float(me[s][0]))
    for k, s in enumerate(two(r)):
        vz = act([k3], T.vz[:, H * k:H * k + H], T.ir[:, 0:H], Act.Identity, bias=float(me[s][0]))
    if z is not None:
        zi = act([k3], T.zi[:], T.ir[:, 0:H], Act.Identity, bias=float(me[z][0]))
    sxu = tc([sx], T.su[:], T.sx[:])
    ks = tc([sxu, kr], T.kr[:].indirect(T.su[:, 14:26]), T.ir[:, 0:C])
    if hi2 is not None:
        l2 = ts([f2, j0], T.l2[:, 0:7], T.tj[:, 0:7], T.f2[:], Op.add)
    kd = diag([ks, mk], T.kd[:], T.kr[:, 0:C], C)
    qx = do("v", [dx], lambda: V.quantize_mx(T.raw[:, 0:C], T.raws[:, 0:C], T.xt[:, 0:4 * C]))

    ma, pa = me[r][0], seg(pt)[r][0]
    pb = do("g", [drow], lambda: g.partition_broadcast(T.row[:], T.row1[0:1, :], 128))
    fused([sxu], [([pt], E, "apt", T.su[:, 0:12], [T.pt[:]])])
    dma("s", "down", codes(T.win[:, ma:ma + C]), codes(T.raw[:, 0:C]), [qx])
    down = dma("s", "down", T.wins[:, ma:ma + C], T.raws[:, 0:C], [qx])

    kl = ts([kd], T.kl[:], T.kd[:, 15:C:16], C - 1.0, Op.min)
    ke = tc([kd], T.ke[:], T.kd[:, 15:C:16])
    er = scan([pb], T.er[:, 1:C], T.row[:, 0:C - 1], T.row[:, 0:C - 1], 0.0, Op.add, Op.max)
    cq = pick([kl, qx], T.comp[:, 0:C], T.raw[:, 0:C], T.kl[:, 0:12])
    cs = act([kl, qx], T.comps[:, 0:C], T.raws[:, 0:C].indirect(T.kl[:, 0:12]))
    sc = act([er, e0, ep, ke], T.sc[:, 0:C], T.er[:, 0:2 * C].indirect(T.ke[:, 0:12]))
    src, scl, tabs, tk = {}, {}, {}, {}
    if hi2 is not None:
        q2 = pick([l2, cq], T.sel2[:, 0:H], T.comp[:, 0:C], T.l2[:, 0:7])
        src[hi2] = (T.sel2, q2)
        r2 = act([sc, l2], T.r2[:], T.sc[:, 0:C].indirect(T.l2[:, 0:7]))
    if lo2 is not None:
        src[lo2] = (T.comp, cq)
    at = {d: seg(d)[r][0] for d in seg(r)}
    fused([src[d][1] for d in two(r)], [([d], share(r, d), "acd", codes(src[d][0][:, 0:H]), [codes(T.win[:, at[d]:at[d] + H])]) for d in two(r)])
    fused([qx], [([pt], inner(r), "apc", codes(T.raw[:, 0:C]), [codes(T.win[:, pa:pa + C])])])
    fused([qx], [([pt], inner(r), "apc", T.raws[:, 0:C], [T.wins[:, pa:pa + C]])])

    na = sum(len(eng(s)) for s in range(N) if s != r and slot(s, r) is not None)
    a, b = half - len(summed(r)), half + 1 if r < half else half + 2
    tS = act([fs] + ([("atot", na)] if na else []), T.js[:, 0:b - a], T.tl[:, a:b], scale=1.0 if r < half else -1.0, accum_out=T.S[:])
    if z is not None:
        ac = act([tS, sc], T.jk[:, 0:C - H], T.sc[:, 1:C - H + 1], Act.Sign, bias=T.S[:], accum_out=T.acc[:])
    if pt > r:
        pc = act([tS, ee], T.pc[:], T.ee[:, 12:13], Act.Identity, bias=T.S[:])
    else:
        pc = act([tS], T.pc[:], T.tl[:, slot(pt, r):slot(pt, r) + 1], Act.Identity, scale=-1.0, bias=T.S[:])
    if lo2 is not None:
        tabs[lo2] = (T.t0, T.d0, diag([sc], T.d0[:], T.sc[:, 0:H], H))
    if hi2 is not None:
        tabs[hi2] = (T.t2, T.d2, diag([r2], T.d2[:], T.r2[:], H))
    qw = [quant(0, 384, dw0), quant(384, 768, dw1)]

    if z is not None:
        le = ts([ac, j3], T.lze[:, 0:7], T.m2[:, 0:7], T.acc[:], Op.add, -0.5, Op.mult)
        rz = act([le], T.rz[:], T.sc[:, 0:C].indirect(T.lze[:, 0:7]))
    if lo2 is not None:
        scl[lo2] = (T.comps, cs)
    if hi2 is not None:
        scl[hi2] = (T.sel2s, act([l2, cs], T.sel2s[:, 0:H], T.comps[:, 0:C].indirect(T.l2[:, 0:7])))
    if z is not None:
        qzs = act([le, cs], T.selzs[:, 0:H], T.comps[:, 0:C].indirect(T.lze[:, 0:7]))
    for d in tabs:
        t, dd, tok = tabs[d]
        tk[d] = ts([tok, tS], t[:, 0:7], dd[:, 15:H:16], T.S[:], Op.add, base(d), Op.add)
    fused([tk[d] for d in two(r)], [([d], share(r, d), "act", tabs[d][0][:, 0:7], [T.ct[:, 7 * two(d).index(r):7 * two(d).index(r) + 7]]) for d in two(r)])
    if z is not None:
        qz = pick([le, cq], T.selz[:, 0:H], T.comp[:, 0:C], T.lze[:, 0:7])
        u = diag([rz], T.dz[:], T.rz[:], H)
    oo = ts([tS, sx], T.po[:, 0:12], T.sx[:, 0:12], T.S[:], Op.add, base(r), Op.add)
    if z is not None:
        tz = ts([u], T.tz[:, 0:7], T.dz[:, 15:H:16], T.S[:], Op.add, base(z), Op.add)
        fused([tz], [([z], E, "acz", T.tz[:, 0:7], [T.cz[:, 0:7]])])
        fused([qz], [([z], E, "acd", codes(T.selz[:, 0:H]), [codes(T.win[:, at[z]:at[z] + H])])])
    fused([scl[d][1] for d in two(r)], [([d], share(r, d), "acd", scl[d][0][:, 0:H], [T.wins[:, at[d]:at[d] + H]]) for d in two(r)])
    if z is not None:
        fused([qzs], [([z], E, "acd", T.selzs[:, 0:H], [T.wins[:, at[z]:at[z] + H]])])

    po = ts([pc, ("apt", len(eng(pt)))], T.po[:, 12:24], T.pt[:], T.pc[:], Op.add, base(r), Op.add)
    pp = tc([oo, po, fp, op], T.pw[:].indirect(T.po[:, 0:24]), T.op[:])
    nt = len(two(r))
    pp = tc([pp, vz, ("act", sum(len(share(s, r)) for s in two(r)))], T.pw[:].indirect(T.ct[:, 0:7 * nt]), T.vz[:, 0:H * nt])
    if z is not None:
        pp = tc([pp, zi, ("acz", len(eng(z)))], T.pw[:].indirect(T.cz[:, 0:7]), T.zi[:])

    ncd = sum(2 * len(share(s, r)) for s in two(r)) + (2 * len(eng(z)) if z is not None else 0)
    got = [down, ("apc", 2 * len(inner(pt))), ("acd", ncd)]

    X = slice(W0 - 16, W0 + P)
    m = scan([pp], T.pm[:], T.pw[:, X], T.pw[:, X], 0.0, Op.max, Op.max)
    d0 = diag([m], T.pd[:, 0:128], T.pm[:, 16:144], 128)
    d1 = diag([m], T.pd[:, 128:P], T.pm[:, 144:16 + P], P - 128)
    l0 = tc([d0], T.il[:, 0:8], T.pd[:, 15:128:16])
    l1 = tc([d1], T.il[:, 8:24], T.pd[:, 143:P:16])

    def fin(b):
        i = slice(128 * b, 128 * b + 128)
        o = T.il[:, 8 * b:8 * b + 8]
        dep = [l1 if b else l0] + got
        return [pick(dep, T.fin[:, i], T.win[:], o), act(dep, T.fins[:, i], T.wins[:].indirect(o))]

    def mul(b, h, deps):
        k = NO * b + h
        wi = slice(128 * k, 128 * k + 128)
        i = slice(128 * b, 128 * b + 128)
        return do("t", deps + qw, lambda: g.tensor.matmul_mx(
            T.ps[:, 512 * k:512 * k + 128], T.wq[:, wi], T.ws[:, wi], T.fin[:, i], T.fins[:, i], True, True))

    def out(b, h, mm):
        k = NO * b + h
        yi = slice(P * h + 128 * b, P * h + 128 * b + 128)
        cp = tc([mm], T.ysb[:, yi], T.ps[:, 512 * k:512 * k + 128]) if h == 0 else act([mm], T.ysb[:, yi], T.ps[:, 512 * k:512 * k + 128])
        dma("s", "dy", T.y[:, yi], T.ysb[:, yi], [cp])

    y = []
    for b in range(NB):
        c = fin(b)
        y.append([mul(b, h, c) for h in range(NO)])
    for b in range(NB):
        for h in range(NO):
            out(b, h, y[b][h])

    need("s", [("dy", total["dy"])])
    g.wait_ge(T.sem.sent, sent[0])
    need("g", [(s, total[s]) for s in total if s != "dy"])
